import numpy as np
import ml_dtypes


def mxq(x, axis, fmt="e4m3"):
    dtype, down = {"e4m3": (ml_dtypes.float8_e4m3fn, 7), "e5m2": (ml_dtypes.float8_e5m2, 14)}[fmt]
    v = np.moveaxis(np.asarray(x, np.float32).astype(ml_dtypes.bfloat16).astype(np.float64), axis, -1)
    blocks = v.reshape(v.shape[:-1] + (-1, 32))
    amax = np.abs(blocks).max(-1, keepdims=True)
    byte = np.maximum(np.where(amax > 0, np.frexp(amax)[1] - 1 + 127, 0) - down, 1)
    scale = np.exp2(byte - 127.0)
    codes = (blocks / scale).astype(np.float32).astype(dtype).astype(np.float64)
    return np.moveaxis((codes * scale).reshape(v.shape), -1, axis)


WIDE = False


def mx_kscale(k):
    if not WIDE:
        return np.ones(k)
    levels = np.array([10, -10, 5, -5, 0])
    if k % 512:
        return np.exp2(np.random.permutation(np.resize(levels, k // 32))).repeat(32)
    a = np.empty((k // 512, 16))
    for p in range(k // 512):
        a[p, :8] = np.random.permutation(np.resize(levels, 8))
        for g in range(8):
            far = levels[np.abs(levels - a[p, g]) >= 10]
            a[p, g + 8] = far[np.random.randint(len(far))]
    return np.exp2(a.ravel()).repeat(32)


def f64(x):
    return np.asarray(x).astype(np.float64)


def striped(idx):
    return np.tile(idx.reshape(-1, 16).T, (8, 1)).astype(np.uint16)


def unstriped(offs):
    return offs[:16].T.reshape(-1).astype(np.int64)


def striped8(idx):
    return np.concatenate([x.reshape(-1, 16).T for x in idx]).astype(np.uint16)


def runs(offs, k):
    lists = np.stack([offs[16 * r : 16 * r + 16].T.reshape(-1) for r in range(8)]).astype(np.int64)
    return lists[np.arange(k) % 512 // 64]


def pack_weight(w):
    k, n = w.shape
    w = f64(np.asarray(w, np.float32).astype(ml_dtypes.bfloat16)).reshape(k // 32, 32, n)
    amax = np.abs(w).max(1)
    byte = np.clip(np.where(amax > 0, np.frexp(amax)[1] - 1 + 127 - 7, 1), 1, 254)
    scaled = (w * np.exp2(127.0 - byte)[:, None, :]).reshape(k, n).astype(np.float32)
    words = np.ascontiguousarray(scaled.reshape(k // 512, 128, 4, n).transpose(0, 1, 3, 2)).astype(ml_dtypes.float8_e4m3fn).view(np.uint8)
    return words, np.ascontiguousarray(byte.astype(np.uint8).reshape(k // 512, 16, n))


def unpack_weight(words, scales):
    g, p, n, _ = words.shape
    vals = np.ascontiguousarray(words).view(ml_dtypes.float8_e4m3fn).astype(np.float64) * np.repeat(np.exp2(scales.astype(np.float64) - 127.0), 8, axis=1)[..., None]
    return vals.transpose(0, 1, 3, 2).reshape(g * 512, n)


E2M1 = np.array([0.0, 0.5, 1.0, 1.5, 2.0, 3.0, 4.0, 6.0, -0.0, -0.5, -1.0, -1.5, -2.0, -3.0, -4.0, -6.0])


def pack_fp4(w):
    k, n = w.shape
    w = f64(np.asarray(w, np.float32).astype(ml_dtypes.bfloat16)).reshape(k // 32, 32, n)
    amax = np.abs(w).max(1)
    mant, ex = np.frexp(amax / 6.0)
    byte = np.clip(np.where(amax > 0, np.where(mant > 0.5, ex, ex - 1) + 127, 1), 1, 254)
    scaled = (w * np.exp2(127.0 - byte)[:, None, :]).reshape(k, n).astype(np.float32)
    c = np.ascontiguousarray(scaled.reshape(k // 512, 128, 4, n).transpose(0, 1, 3, 2)).astype(ml_dtypes.float4_e2m1fn).view(np.uint8) & 0xF
    words = (c[..., 0::2] | (c[..., 1::2] << 4)).reshape(k // 512, 128, 2 * n)
    return np.ascontiguousarray(words), np.ascontiguousarray(byte.astype(np.uint8).reshape(k // 512, 16, n))


def unpack_fp4(words, scales):
    g, _, n = scales.shape
    words = np.ascontiguousarray(words).reshape(g, 128, n, 2)
    nib = np.empty((g, 128, n, 4), np.uint8)
    nib[..., 0::2] = words & 0xF
    nib[..., 1::2] = words >> 4
    vals = E2M1[nib] * np.repeat(np.exp2(scales.astype(np.float64) - 127.0), 8, axis=1)[..., None]
    return vals.transpose(0, 1, 3, 2).reshape(g * 512, n)


def sigmoid(v):
    return 1.0 / (1.0 + np.exp(-np.maximum(v, -700.0)))

def planes(y):
    n, m = y.shape
    v = y.astype(np.float32).astype(ml_dtypes.bfloat16).astype(np.float64).reshape(n // 32, 32, m)
    top = np.abs(v).max(1)
    byte = np.clip(np.where(top > 0, np.frexp(top)[1] - 1 + 127 - 7, 1), 1, 254)
    codes = (v * np.exp2(127.0 - byte)[:, None, :]).reshape(n, m).astype(np.float32).astype(ml_dtypes.float8_e4m3fn).view(np.uint8)
    words = codes.reshape(n // 512, 128, 4, m).transpose(0, 1, 3, 2)
    return np.ascontiguousarray(words), np.ascontiguousarray(byte.astype(np.uint8).reshape(n // 512, 16, m))


K, T, S, N, H = 512, 2048, 512, 512, 512


def setup_inputs():
    n = np.random.standard_normal
    s = mx_kscale(K)[:, None]
    u = mx_kscale(H)
    packed_xT = pack_weight(n((K, T)) * s)
    packed_w1 = pack_fp4(n((K, H)) / np.sqrt(K) / s)
    packed_w2 = pack_fp4(n((H, N)) / np.sqrt(2 * H) / u[:, None])
    packed_w3 = pack_fp4(n((H, N)) / np.sqrt(2 * H) / u[:, None])
    return {
        "x_words": packed_xT[0],
        "x_scales": packed_xT[1],
        "w1_words": packed_w1[0],
        "w1_scales": packed_w1[1],
        "gn": (np.random.uniform(0.5, 1.5, (H, 1)) * u[:, None]).astype(np.float32),
        "gm": (np.random.uniform(0.5, 1.5, (H, 1)) * u[:, None]).astype(np.float32),
        "w2_words": packed_w2[0],
        "w2_scales": packed_w2[1],
        "w3_words": packed_w3[0],
        "w3_scales": packed_w3[1],
        "offs": striped(np.random.permutation(T)[:S]),
        "n1": striped8(np.stack([np.random.permutation(S) for _ in range(8)])),
        "n2": striped8(np.stack([np.random.permutation(S) for _ in range(8)])),
        "n3": striped8(np.stack([np.random.permutation(S) for _ in range(8)])),
        "n4": striped8(np.stack([np.random.permutation(S) for _ in range(8)])),
    }


def reference(x_words, x_scales, w1_words, w1_scales, gn, gm, w2_words, w2_scales, w3_words, w3_scales, offs, n1, n2, n3, n4):
    xq = unpack_weight(x_words, x_scales)[:, unstriped(offs)]
    y = unpack_fp4(w1_words, w1_scales).T @ xq
    z = f64(gn) * (y * (sigmoid(y[np.arange(H)[:, None], runs(n1, H)])))
    ex = np.exp(y)
    z2 = f64(gm) * (np.log(ex + ex[np.arange(H)[:, None], runs(n2, H)]) - (y[np.arange(H)[:, None], runs(n3, H)]))
    h = unpack_fp4(w2_words, w2_scales).T @ mxq(z, 0, "e4m3") + unpack_fp4(w3_words, w3_scales).T @ mxq(z2, 0, "e4m3")
    pa = h[np.arange(N)[:, None], runs(n4, N)]
    out_0 = (2.0 * (h * pa)) / ((h) ** 2 + (pa) ** 2 + 0.5)
    return (out_0,) + planes(out_0)

@@ -1,0 +1,217 @@
+from contextlib import ExitStack
+
+import concourse.mybir as mybir
+
+K, T, S, N, H = 512, 2048, 512, 512, 512
+FLOPS = 3 * 2 * 512 * 512 * 512
+
+F32 = mybir.dt.float32
+BF16 = mybir.dt.bfloat16
+I32 = mybir.dt.int32
+U32 = mybir.dt.uint32
+U16 = mybir.dt.uint16
+U8 = mybir.dt.uint8
+FP8X4 = mybir.dt.float8_e4m3fn_x4
+FP4X4 = mybir.dt.float4_e2m1fn_x4
+ALU = mybir.AluOpType
+ACT = mybir.ActivationFunctionType
+
+P = 128
+PACK = 4
+HALF = S // 2
+
+
+def tile_picked_joingatelseharm_none_po_kernel(
+    tc, x_words, x_scales, w1_words, w1_scales, gn, gm, w2_words, w2_scales, w3_words, w3_scales,
+    offs, n1, n2, n3, n4, out_0, out_1, out_2,
+):
+    nc = tc.nc
+    with ExitStack() as ctx:
+        keep = ctx.enter_context(tc.tile_pool(name="keep", bufs=1))
+        psum = ctx.enter_context(tc.psum_pool(name="psum", bufs=1))
+
+        def tile(name, shape, dtype):
+            return keep.tile(shape, dtype, name=name, align_bytes=64)
+
+        def load_list(name, src):
+            lst = keep.tile([P, S // 16], U16, name=name)
+            nc.sync.dma_start(lst[:], src)
+            return lst
+
+        def load_scale_rows(queue, dst, src):
+            for q in range(4):
+                queue.dma_start(dst[32 * q : 32 * q + 4, :].bitcast(I32), src[0, 4 * q : 4 * q + 4, :].bitcast(I32))
+
+        def deal_words(name, raw):
+            dealt = tile(name, [P, PACK, 2 * P], U8)
+            nc.vector.tensor_copy(
+                dealt[:].rearrange("p t (m b) -> p t m b", b=2),
+                raw[:].rearrange("p (m t b) -> p t m b", t=PACK, b=2),
+            )
+            return dealt
+
+        def deal_scales(name, raw):
+            dealt = tile(name, [P, PACK, P], U8)
+            nc.vector.tensor_copy(dealt[:], raw[:].rearrange("p (m t) -> p t m", t=PACK))
+            return dealt
+
+        def interleave(dst, src):
+            nc.vector.tensor_copy(
+                dst.rearrange("p (c i) t -> p c t i", i=4),
+                src.rearrange("p t (c i) -> p c t i", i=4),
+            )
+
+        def cols(lst, lo, n):
+            return lst[:, lo // 16 : (lo + n) // 16]
+
+        xs_raw = tile("xs_raw", [P, T], U8)
+        nc.gpsimd.memset(xs_raw[:].bitcast(I32), 0)
+        w1s_raw = tile("w1s_raw", [P, H], U8)
+        nc.gpsimd.memset(w1s_raw[:].bitcast(I32), 0)
+        w2s_raw = tile("w2s_raw", [P, N], U8)
+        nc.vector.memset(w2s_raw[:].bitcast(I32), 0)
+        w3s_raw = tile("w3s_raw", [P, N], U8)
+        nc.vector.memset(w3s_raw[:].bitcast(I32), 0)
+
+        offs_t = load_list("offs_t", offs)
+        w1_raw = tile("w1_raw", [P, 2 * H], U8)
+        nc.sync.dma_start(w1_raw[:].bitcast(I32), w1_words[0].bitcast(I32))
+        n1_t = load_list("n1_t", n1)
+        xw_raw = tile("xw_raw", [P, T], I32)
+        nc.sync.dma_start(xw_raw[:], x_words[0].rearrange("p n t -> p (n t)").bitcast(I32))
+        load_scale_rows(nc.sync, xs_raw, x_scales)
+        for q in range(3):
+            nc.sync.dma_start(w1s_raw[32 * q : 32 * q + 4, :].bitcast(I32), w1_scales[0, 4 * q : 4 * q + 4, :].bitcast(I32))
+        nc.gpsimd.dma_start(w1s_raw[96:100, :].bitcast(I32), w1_scales[0, 12:16, :].bitcast(I32))
+        w2_raw = tile("w2_raw", [P, 2 * N], U8)
+        nc.gpsimd.dma_start(w2_raw[:].bitcast(I32), w2_words[0].bitcast(I32))
+        w3_raw = tile("w3_raw", [P, 2 * N], U8)
+        nc.gpsimd.dma_start(w3_raw[:].bitcast(I32), w3_words[0].bitcast(I32))
+        gn_t = tile("gn_t", [P, PACK], F32)
+        nc.gpsimd.dma_start(gn_t[:], gn.rearrange("(p t) o -> p (t o)", t=PACK))
+        gm_t = tile("gm_t", [P, PACK], F32)
+        nc.gpsimd.dma_start(gm_t[:], gm.rearrange("(p t) o -> p (t o)", t=PACK))
+        n2_t = load_list("n2_t", n2)
+        n3_t = load_list("n3_t", n3)
+        load_scale_rows(nc.sync, w2s_raw, w2_scales)
+        load_scale_rows(nc.sync, w3s_raw, w3_scales)
+        n4_t = load_list("n4_t", n4)
+
+        w1_c = deal_words("w1_c", w1_raw)
+        xs = tile("xs", [P, S], U8)
+        nc.vector.tensor_copy(xs[:], xs_raw[:].indirect(offs_t[:]))
+        w1_s = deal_scales("w1_s", w1s_raw)
+        xw = [tile("xw%d" % c, [P, HALF], U32) for c in range(2)]
+        for c in range(2):
+            nc.vector.tensor_copy(xw[c][:], xw_raw[:].bitcast(U32).indirect(cols(offs_t, c * HALF, HALF)))
+
+        y_ps = [psum.tile([P, S], F32, name="y_ps%d" % t) for t in range(PACK)]
+        for c in range(2):
+            for t in range(PACK):
+                nc.tensor.matmul_mx(
+                    out=y_ps[t][:, c * HALF : (c + 1) * HALF], lhsT=w1_c[:, t, :].bitcast(FP4X4), lhsT_scale=w1_s[:, t, :],
+                    rhs=xw[c][:].bitcast(FP8X4), rhs_scale=xs[:, c * HALF : (c + 1) * HALF], start=True, stop=True,
+                )
+        w2_c = deal_words("w2_c", w2_raw)
+        w3_c = deal_words("w3_c", w3_raw)
+
+        th = [tile("th%d" % t, [P, S], F32) for t in range(PACK)]
+        yex = [tile("yex%d" % t, [P, 2 * S], F32) for t in range(PACK)]
+        sg = [tile("sg%d" % t, [P, S], F32) for t in range(PACK)]
+        e2 = [tile("e2_%d" % t, [P, S], F32) for t in range(PACK)]
+        sums = tile("sums", [P, PACK, S], F32)
+        z_p = tile("z_p", [P, PACK, S], BF16)
+        for t in range(PACK):
+            nc.scalar.activation(th[t][:], y_ps[t][:], ACT.Tanh, scale=0.5)
+            nc.scalar.copy(yex[t][:, :S], y_ps[t][:])
+            nc.scalar.activation(yex[t][:, S:], y_ps[t][:], ACT.Exp)
+            nc.scalar.activation(e2[t][:], yex[t][:].indirect(n2_t[:]), ACT.Exp)
+            for c in range(2):
+                nc.vector.tensor_scalar(
+                    sg[t][:, c * HALF : (c + 1) * HALF], th[t][:].indirect(cols(n1_t, c * HALF, HALF)),
+                    0.5, 0.5, ALU.mult, ALU.add,
+                )
+            nc.vector.scalar_tensor_tensor(z_p[:, t, :], y_ps[t][:], gn_t[:, t : t + 1], sg[t][:], ALU.mult, ALU.mult)
+            nc.vector.tensor_tensor(sums[:, t, :], yex[t][:, S:], e2[t][:], ALU.add)
+
+        z_i = tile("z_i", [P, S, PACK], BF16)
+        interleave(z_i[:], z_p[:])
+        w2_s = deal_scales("w2_s", w2s_raw)
+        z_c = tile("z_c", [P, S], U32)
+        z_s = tile("z_s", [P, S], U8)
+        nc.vector.quantize_mx(z_c[:].bitcast(FP8X4), z_s[:], z_i[:].rearrange("p c t -> p (c t)"))
+        w3_s = deal_scales("w3_s", w3s_raw)
+
+        h_ps = [psum.tile([P, S], F32, name="h_ps%d" % t) for t in range(PACK)]
+        for t in range(PACK):
+            nc.tensor.matmul_mx(
+                out=h_ps[t][:], lhsT=w2_c[:, t, :].bitcast(FP4X4), lhsT_scale=w2_s[:, t, :],
+                rhs=z_c[:].bitcast(FP8X4), rhs_scale=z_s[:], start=True, stop=False,
+            )
+
+        ngm = tile("ngm", [P, PACK], F32)
+        nc.scalar.activation(ngm[:], gm_t[:], ACT.Copy, scale=-1.0)
+        z2_c = tile("z2_c", [P, S], U32)
+        z2_s = tile("z2_s", [P, S], U8)
+        lse = [tile("lse%d" % c, [P, PACK, HALF], F32) for c in range(2)]
+        dif = [tile("dif%d" % c, [P, PACK, HALF], F32) for c in range(2)]
+        z2_p = [tile("z2_p%d" % c, [P, PACK, HALF], BF16) for c in range(2)]
+        z2_i = [tile("z2_i%d" % c, [P, HALF, PACK], BF16) for c in range(2)]
+        for c in range(2):
+            nc.scalar.activation(lse[c][:], sums[:, :, c * HALF : (c + 1) * HALF], ACT.Ln)
+        for c in range(2):
+            for t in range(PACK):
+                nc.vector.tensor_tensor(
+                    dif[c][:, t, :], yex[t][:].indirect(cols(n3_t, c * HALF, HALF)), lse[c][:, t, :], ALU.subtract
+                )
+                nc.scalar.activation(z2_p[c][:, t, :], dif[c][:, t, :], ACT.Copy, scale=ngm[:, t : t + 1])
+        for c in range(2):
+            interleave(z2_i[c][:], z2_p[c][:])
+            nc.vector.quantize_mx(
+                z2_c[:, c * HALF : (c + 1) * HALF].bitcast(FP8X4), z2_s[:, c * HALF : (c + 1) * HALF],
+                z2_i[c][:].rearrange("p c t -> p (c t)"),
+            )
+        for t in range(PACK):
+            nc.tensor.matmul_mx(
+                out=h_ps[t][:], lhsT=w3_c[:, t, :].bitcast(FP4X4), lhsT_scale=w3_s[:, t, :],
+                rhs=z2_c[:].bitcast(FP8X4), rhs_scale=z2_s[:], start=False, stop=True,
+            )
+
+        h = [tile("h%d" % t, [P, S], F32) for t in range(PACK)]
+        hsq = tile("hsq", [P, PACK, S], F32)
+        for t in range(PACK):
+            nc.scalar.copy(h[t][:], h_ps[t][:])
+        for t in range(PACK):
+            nc.scalar.activation(hsq[:, t, :], h_ps[t][:], ACT.Square)
+        o_c = tile("o_c", [P, S], U32)
+        o_s = tile("o_s", [P, S], U8)
+        out_rows = out_0.rearrange("(p t) c -> p t c", t=PACK)
+        out_words = out_1[0].rearrange("p n t -> p (n t)").bitcast(I32)
+        chunks = [(0, 256), (256, 128), (384, 128)]
+        for lo, n in chunks:
+            pa = tile("pa%d" % lo, [P, PACK, n], F32)
+            num = tile("num%d" % lo, [P, PACK, n], F32)
+            for t in range(PACK):
+                nc.vector.tensor_copy(pa[:, t, :], h[t][:].indirect(cols(n4_t, lo, n)))
+            pasq = tile("pasq%d" % lo, [P, PACK, n], F32)
+            nc.scalar.activation(pasq[:], pa[:], ACT.Square)
+            for t in range(PACK):
+                nc.vector.tensor_tensor(num[:, t, :], h_ps[t][:, lo : lo + n], pa[:, t, :], ALU.mult)
+            den = tile("den%d" % lo, [P, PACK, n], F32)
+            nc.vector.scalar_tensor_tensor(den[:], hsq[:, :, lo : lo + n], 0.5, pasq[:], ALU.add, ALU.add)
+            rs = tile("rs%d" % lo, [P, PACK, n], F32)
+            nc.scalar.activation(rs[:], den[:], ACT.Abs_reciprocal_sqrt, scale=0.5)
+            rec = tile("rec%d" % lo, [P, PACK, n], F32)
+            nc.scalar.activation(rec[:], rs[:], ACT.Square)
+            res = tile("res%d" % lo, [P, PACK, n], F32)
+            nc.vector.tensor_tensor(res[:], num[:], rec[:], ALU.mult)
+            nc.sync.dma_start(out_rows[:, :, lo : lo + n], res[:])
+            res_i = tile("res_i%d" % lo, [P, n, PACK], BF16)
+            interleave(res_i[:], res[:])
+            nc.vector.quantize_mx(
+                o_c[:, lo : lo + n].bitcast(FP8X4), o_s[:, lo : lo + n], res_i[:].rearrange("p c t -> p (c t)")
+            )
+            nc.sync.dma_start(out_words[:, lo : lo + n], o_c[:, lo : lo + n].bitcast(I32))
+        for q in range(4):
+            queue = nc.scalar if q % 2 else nc.sync
+            queue.dma_start(out_2[0, 4 * q : 4 * q + 4, :].bitcast(I32), o_s[32 * q : 32 * q + 4, :].bitcast(I32))

@@ -1,6 +1,7 @@
 from contextlib import ExitStack
 
 import concourse.mybir as mybir
+from concourse.masks import make_identity
 
 K, T, S, N, H = 512, 2048, 512, 512, 512
 FLOPS = 3 * 2 * 512 * 512 * 512
@@ -30,8 +31,8 @@ def tile_picked_joingatelseharm_none_po_kernel(
         keep = ctx.enter_context(tc.tile_pool(name="keep", bufs=1))
         psum = ctx.enter_context(tc.psum_pool(name="psum", bufs=1))
 
-        def tile(name, shape, dtype):
-            return keep.tile(shape, dtype, name=name, align_bytes=64)
+        def tile(name, shape, dtype, tag=None):
+            return keep.tile(shape, dtype, name=name, tag=tag or name, align_bytes=64)
 
         def load_list(name, src):
             lst = keep.tile([P, S // 16], U16, name=name)
@@ -45,8 +46,8 @@ def tile_picked_joingatelseharm_none_po_kernel(
         def deal_words(name, raw):
             dealt = tile(name, [P, PACK, 2 * P], U8)
             nc.vector.tensor_copy(
-                dealt[:].rearrange("p t (m b) -> p t m b", b=2),
-                raw[:].rearrange("p (m t b) -> p t m b", t=PACK, b=2),
+                dealt[:].rearrange("p t (m b) -> p m t b", b=2),
+                raw[:].rearrange("p (m t b) -> p m t b", t=PACK, b=2),
             )
             return dealt
 
@@ -65,13 +66,16 @@ def tile_picked_joingatelseharm_none_po_kernel(
             return lst[:, lo // 16 : (lo + n) // 16]
 
         xs_raw = tile("xs_raw", [P, T], U8)
-        nc.gpsimd.memset(xs_raw[:].bitcast(I32), 0)
+        nc.vector.memset(xs_raw[:].bitcast(I32), 0)
         w1s_raw = tile("w1s_raw", [P, H], U8)
         nc.gpsimd.memset(w1s_raw[:].bitcast(I32), 0)
         w2s_raw = tile("w2s_raw", [P, N], U8)
         nc.vector.memset(w2s_raw[:].bitcast(I32), 0)
         w3s_raw = tile("w3s_raw", [P, N], U8)
         nc.vector.memset(w3s_raw[:].bitcast(I32), 0)
+
+        def load_scale_quadrant(queue, dst, src, q):
+            queue.dma_start(dst[32 * q : 32 * q + 4, :].bitcast(I32), src[0, 4 * q : 4 * q + 4, :].bitcast(I32))
 
         offs_t = load_list("offs_t", offs)
         w1_raw = tile("w1_raw", [P, 2 * H], U8)
@@ -81,39 +85,46 @@ def tile_picked_joingatelseharm_none_po_kernel(
         nc.sync.dma_start(xw_raw[:], x_words[0].rearrange("p n t -> p (n t)").bitcast(I32))
         load_scale_rows(nc.sync, xs_raw, x_scales)
         for q in range(3):
-            nc.sync.dma_start(w1s_raw[32 * q : 32 * q + 4, :].bitcast(I32), w1_scales[0, 4 * q : 4 * q + 4, :].bitcast(I32))
-        nc.gpsimd.dma_start(w1s_raw[96:100, :].bitcast(I32), w1_scales[0, 12:16, :].bitcast(I32))
-        w2_raw = tile("w2_raw", [P, 2 * N], U8)
-        nc.gpsimd.dma_start(w2_raw[:].bitcast(I32), w2_words[0].bitcast(I32))
-        w3_raw = tile("w3_raw", [P, 2 * N], U8)
-        nc.gpsimd.dma_start(w3_raw[:].bitcast(I32), w3_words[0].bitcast(I32))
+            load_scale_quadrant(nc.sync, w1s_raw, w1_scales, q)
+        load_scale_quadrant(nc.gpsimd, w1s_raw, w1_scales, 3)
         gn_t = tile("gn_t", [P, PACK], F32)
         nc.gpsimd.dma_start(gn_t[:], gn.rearrange("(p t) o -> p (t o)", t=PACK))
         gm_t = tile("gm_t", [P, PACK], F32)
         nc.gpsimd.dma_start(gm_t[:], gm.rearrange("(p t) o -> p (t o)", t=PACK))
+        ident = tile("ident", [P, P], F32)
+        make_identity(nc, ident[:])
+        w2_raw = tile("w2_raw", [P, 2 * N], U8)
+        nc.sync.dma_start(w2_raw[:].bitcast(I32), w2_words[0].bitcast(I32))
         n2_t = load_list("n2_t", n2)
+        w3_raw = tile("w3_raw", [P, 2 * N], U8)
+        nc.sync.dma_start(w3_raw[:].bitcast(I32), w3_words[0].bitcast(I32))
         n3_t = load_list("n3_t", n3)
+        n4_t = load_list("n4_t", n4)
         load_scale_rows(nc.sync, w2s_raw, w2_scales)
         load_scale_rows(nc.sync, w3s_raw, w3_scales)
-        n4_t = load_list("n4_t", n4)
 
         w1_c = deal_words("w1_c", w1_raw)
-        xs = tile("xs", [P, S], U8)
-        nc.vector.tensor_copy(xs[:], xs_raw[:].indirect(offs_t[:]))
-        w1_s = deal_scales("w1_s", w1s_raw)
+        xs = [tile("xs%d" % c, [P, HALF], U8) for c in range(2)]
         xw = [tile("xw%d" % c, [P, HALF], U32) for c in range(2)]
-        for c in range(2):
+
+        def pick_words(c):
             nc.vector.tensor_copy(xw[c][:], xw_raw[:].bitcast(U32).indirect(cols(offs_t, c * HALF, HALF)))
 
-        y_ps = [psum.tile([P, S], F32, name="y_ps%d" % t) for t in range(PACK)]
-        for c in range(2):
-            for t in range(PACK):
-                nc.tensor.matmul_mx(
-                    out=y_ps[t][:, c * HALF : (c + 1) * HALF], lhsT=w1_c[:, t, :].bitcast(FP4X4), lhsT_scale=w1_s[:, t, :],
-                    rhs=xw[c][:].bitcast(FP8X4), rhs_scale=xs[:, c * HALF : (c + 1) * HALF], start=True, stop=True,
-                )
-        w2_c = deal_words("w2_c", w2_raw)
-        w3_c = deal_words("w3_c", w3_raw)
+        def pick_scales(c):
+            nc.vector.tensor_copy(xs[c][:], xs_raw[:].indirect(cols(offs_t, c * HALF, HALF)))
+
+        pick_words(0)
+        pick_scales(0)
+        w1_s = deal_scales("w1_s", w1s_raw)
+        pick_words(1)
+        pick_scales(1)
+
+        y_ps = [psum.tile([P, S], F32, name="y_ps%d" % t, tag="bank%d" % t) for t in range(PACK)]
+        for c, t in ((0, 0), (1, 0), (0, 1), (1, 1), (0, 2), (1, 2), (0, 3), (1, 3)):
+            nc.tensor.matmul_mx(
+                out=y_ps[t][:, c * HALF : (c + 1) * HALF], lhsT=w1_c[:, t, :].bitcast(FP4X4), lhsT_scale=w1_s[:, t, :],
+                rhs=xw[c][:].bitcast(FP8X4), rhs_scale=xs[c][:], start=True, stop=True,
+            )
 
         th = [tile("th%d" % t, [P, S], F32) for t in range(PACK)]
         yex = [tile("yex%d" % t, [P, 2 * S], F32) for t in range(PACK)]
@@ -124,16 +135,21 @@ def tile_picked_joingatelseharm_none_po_kernel(
         for t in range(PACK):
             nc.scalar.activation(th[t][:], y_ps[t][:], ACT.Tanh, scale=0.5)
             nc.scalar.copy(yex[t][:, :S], y_ps[t][:])
-            nc.scalar.activation(yex[t][:, S:], y_ps[t][:], ACT.Exp)
-            nc.scalar.activation(e2[t][:], yex[t][:].indirect(n2_t[:]), ACT.Exp)
             for c in range(2):
                 nc.vector.tensor_scalar(
                     sg[t][:, c * HALF : (c + 1) * HALF], th[t][:].indirect(cols(n1_t, c * HALF, HALF)),
                     0.5, 0.5, ALU.mult, ALU.add,
                 )
-            nc.vector.scalar_tensor_tensor(z_p[:, t, :], y_ps[t][:], gn_t[:, t : t + 1], sg[t][:], ALU.mult, ALU.mult)
+            nc.vector.scalar_tensor_tensor(z_p[:, t, :], yex[t][:, :S], gn_t[:, t : t + 1], sg[t][:], ALU.mult, ALU.mult)
+        for t in range(PACK):
+            nc.scalar.activation(yex[t][:, S:], y_ps[t][:], ACT.Exp)
+            nc.scalar.activation(e2[t][:], yex[t][:].indirect(n2_t[:]), ACT.Exp)
             nc.vector.tensor_tensor(sums[:, t, :], yex[t][:, S:], e2[t][:], ALU.add)
 
+        ngm = tile("ngm", [P, PACK], F32)
+        nc.scalar.activation(ngm[:], gm_t[:], ACT.Copy, scale=-1.0)
+        w2_c = deal_words("w2_c", w2_raw)
+        w3_c = deal_words("w3_c", w3_raw)
         z_i = tile("z_i", [P, S, PACK], BF16)
         interleave(z_i[:], z_p[:])
         w2_s = deal_scales("w2_s", w2s_raw)
@@ -142,76 +158,130 @@ def tile_picked_joingatelseharm_none_po_kernel(
         nc.vector.quantize_mx(z_c[:].bitcast(FP8X4), z_s[:], z_i[:].rearrange("p c t -> p (c t)"))
         w3_s = deal_scales("w3_s", w3s_raw)
 
-        h_ps = [psum.tile([P, S], F32, name="h_ps%d" % t) for t in range(PACK)]
-        for t in range(PACK):
-            nc.tensor.matmul_mx(
-                out=h_ps[t][:], lhsT=w2_c[:, t, :].bitcast(FP4X4), lhsT_scale=w2_s[:, t, :],
-                rhs=z_c[:].bitcast(FP8X4), rhs_scale=z_s[:], start=True, stop=False,
-            )
-
-        ngm = tile("ngm", [P, PACK], F32)
-        nc.scalar.activation(ngm[:], gm_t[:], ACT.Copy, scale=-1.0)
-        z2_c = tile("z2_c", [P, S], U32)
-        z2_s = tile("z2_s", [P, S], U8)
-        lse = [tile("lse%d" % c, [P, PACK, HALF], F32) for c in range(2)]
-        dif = [tile("dif%d" % c, [P, PACK, HALF], F32) for c in range(2)]
+        z2_c = [tile("z2_c%d" % c, [P, HALF], U32) for c in range(2)]
+        z2_s = [tile("z2_s%d" % c, [P, HALF], U8) for c in range(2)]
         z2_p = [tile("z2_p%d" % c, [P, PACK, HALF], BF16) for c in range(2)]
         z2_i = [tile("z2_i%d" % c, [P, HALF, PACK], BF16) for c in range(2)]
-        for c in range(2):
-            nc.scalar.activation(lse[c][:], sums[:, :, c * HALF : (c + 1) * HALF], ACT.Ln)
+        h_ps = [
+            [psum.tile([P, HALF], F32, name="h_ps%d_%d" % (c, t), tag="bank%d" % (PACK * (1 - c) + t)) for t in range(PACK)]
+            for c in range(2)
+        ]
+        hsq = tile("hsq", [P, PACK, S], F32)
+        lse = tile("lse", [P, 2 * PACK, HALF], F32, tag="e2_3")
+
+        def log_branch(c, t):
+            dif = tile("dif%d_%d" % (c, t), [P, HALF], F32, tag={(1, 2): "z2_p0", (1, 3): "z2_i0"}.get((c, t)))
+            nc.vector.tensor_tensor(
+                dif[:], yex[t][:].indirect(cols(n3_t, c * HALF, HALF)), lse[:, PACK * c + t, :], ALU.subtract
+            )
+            if PACK * c + t < 6:
+                nc.scalar.activation(z2_p[c][:, t, :], dif[:], ACT.Copy, scale=ngm[:, t : t + 1])
+            else:
+                nc.vector.tensor_scalar(z2_p[c][:, t, :], dif[:], ngm[:, t : t + 1], None, ALU.mult)
+
+        def second_product(c):
+            interleave(z2_i[c][:], z2_p[c][:])
+            nc.vector.quantize_mx(z2_c[c][:].bitcast(FP8X4), z2_s[c][:], z2_i[c][:].rearrange("p c t -> p (c t)"))
+            for t in range(PACK):
+                for b in range(HALF // P):
+                    inner = slice(b * P, (b + 1) * P)
+                    outer = slice(c * HALF + b * P, c * HALF + (b + 1) * P)
+                    nc.tensor.matmul_mx(
+                        out=h_ps[c][t][:, inner], lhsT=w2_c[:, t, :].bitcast(FP4X4), lhsT_scale=w2_s[:, t, :],
+                        rhs=z_c[:, outer].bitcast(FP8X4), rhs_scale=z_s[:, outer], start=True, stop=False,
+                    )
+                    nc.tensor.matmul_mx(
+                        out=h_ps[c][t][:, inner], lhsT=w3_c[:, t, :].bitcast(FP4X4), lhsT_scale=w3_s[:, t, :],
+                        rhs=z2_c[c][:, inner].bitcast(FP8X4), rhs_scale=z2_s[c][:, inner], start=False, stop=True,
+                    )
+
         for c in range(2):
             for t in range(PACK):
-                nc.vector.tensor_tensor(
-                    dif[c][:, t, :], yex[t][:].indirect(cols(n3_t, c * HALF, HALF)), lse[c][:, t, :], ALU.subtract
-                )
-                nc.scalar.activation(z2_p[c][:, t, :], dif[c][:, t, :], ACT.Copy, scale=ngm[:, t : t + 1])
-        for c in range(2):
-            interleave(z2_i[c][:], z2_p[c][:])
-            nc.vector.quantize_mx(
-                z2_c[:, c * HALF : (c + 1) * HALF].bitcast(FP8X4), z2_s[:, c * HALF : (c + 1) * HALF],
-                z2_i[c][:].rearrange("p c t -> p (c t)"),
-            )
+                nc.scalar.activation(lse[:, PACK * c + t, :], sums[:, t, c * HALF : (c + 1) * HALF], ACT.Ln)
         for t in range(PACK):
-            nc.tensor.matmul_mx(
-                out=h_ps[t][:], lhsT=w3_c[:, t, :].bitcast(FP4X4), lhsT_scale=w3_s[:, t, :],
-                rhs=z2_c[:].bitcast(FP8X4), rhs_scale=z2_s[:], start=False, stop=True,
-            )
+            log_branch(0, t)
+        for t in range(2):
+            log_branch(1, t)
+        second_product(0)
+        for t in range(2, PACK):
+            log_branch(1, t)
+        warm = tile("warm", [P, 1], F32)
+        nc.scalar.activation(warm[:], z2_p[1][:, 1, HALF - 1 : HALF], ACT.Abs_reciprocal_sqrt, scale=0.0, bias=1.0)
+        second_product(1)
+        h = [tile("h%d" % t, [P, S], F32, tag=("z2_i1", "z2_p1", "dif1_1", "e2_3")[t]) for t in range(PACK)]
+        for t in range(PACK):
+            nc.scalar.activation(hsq[:, t, :HALF], h_ps[0][t][:], ACT.Square)
+        for t in range(PACK):
+            nc.vector.tensor_copy(h[t][:, :HALF], h_ps[0][t][:])
+        for t in range(PACK):
+            nc.scalar.copy(h[t][:, HALF:], h_ps[1][t][:])
+        for t in range(PACK):
+            nc.scalar.activation(hsq[:, t, HALF:], h_ps[1][t][:], ACT.Square)
 
-        h = [tile("h%d" % t, [P, S], F32) for t in range(PACK)]
-        hsq = tile("hsq", [P, PACK, S], F32)
-        for t in range(PACK):
-            nc.scalar.copy(h[t][:], h_ps[t][:])
-        for t in range(PACK):
-            nc.scalar.activation(hsq[:, t, :], h_ps[t][:], ACT.Square)
         o_c = tile("o_c", [P, S], U32)
         o_s = tile("o_s", [P, S], U8)
         out_rows = out_0.rearrange("(p t) c -> p t c", t=PACK)
         out_words = out_1[0].rearrange("p n t -> p (n t)").bitcast(I32)
-        chunks = [(0, 256), (256, 128), (384, 128)]
-        for lo, n in chunks:
-            pa = tile("pa%d" % lo, [P, PACK, n], F32)
-            num = tile("num%d" % lo, [P, PACK, n], F32)
-            for t in range(PACK):
-                nc.vector.tensor_copy(pa[:, t, :], h[t][:].indirect(cols(n4_t, lo, n)))
-            pasq = tile("pasq%d" % lo, [P, PACK, n], F32)
-            nc.scalar.activation(pasq[:], pa[:], ACT.Square)
-            for t in range(PACK):
-                nc.vector.tensor_tensor(num[:, t, :], h_ps[t][:, lo : lo + n], pa[:, t, :], ALU.mult)
-            den = tile("den%d" % lo, [P, PACK, n], F32)
-            nc.vector.scalar_tensor_tensor(den[:], hsq[:, :, lo : lo + n], 0.5, pasq[:], ALU.add, ALU.add)
-            rs = tile("rs%d" % lo, [P, PACK, n], F32)
-            nc.scalar.activation(rs[:], den[:], ACT.Abs_reciprocal_sqrt, scale=0.5)
-            rec = tile("rec%d" % lo, [P, PACK, n], F32)
-            nc.scalar.activation(rec[:], rs[:], ACT.Square)
-            res = tile("res%d" % lo, [P, PACK, n], F32)
-            nc.vector.tensor_tensor(res[:], num[:], rec[:], ALU.mult)
-            nc.sync.dma_start(out_rows[:, :, lo : lo + n], res[:])
-            res_i = tile("res_i%d" % lo, [P, n, PACK], BF16)
-            interleave(res_i[:], res[:])
-            nc.vector.quantize_mx(
-                o_c[:, lo : lo + n].bitcast(FP8X4), o_s[:, lo : lo + n], res_i[:].rearrange("p c t -> p (c t)")
-            )
-            nc.sync.dma_start(out_words[:, lo : lo + n], o_c[:, lo : lo + n].bitcast(I32))
+        res = tile("res", [P, PACK, S], F32)
+        pa = [tile("pa%d" % t, [P, S], F32) for t in range(PACK)]
+        num = [tile("num%d" % t, [P, S], F32) for t in range(PACK)]
+        den, rec = {}, {}
+
+        def fetch(t):
+            for c in range(2):
+                nc.vector.tensor_copy(pa[t][:, c * HALF : (c + 1) * HALF], h[t][:].indirect(cols(n4_t, c * HALF, HALF)))
+            pasq = tile("pasq%d" % t, [P, S], F32)
+            nc.scalar.activation(pasq[:], pa[t][:], ACT.Square)
+            if t >= 3:
+                den[t] = tile("den%d" % t, [P, S], F32)
+                nc.vector.tensor_tensor(den[t][:], hsq[:, t, :], pasq[:], ALU.add)
+                return
+            den[t] = psum.tile([P, S], F32, name="den_ps%d" % t, tag="bank%d" % (PACK + t))
+            blocks = [slice(b * P, (b + 1) * P) for b in range(S // P)]
+            for b, blk in enumerate(blocks):
+                nc.tensor.matmul(den[t][:, blk], hsq[:, t, blk], ident[:], start=b == 0, stop=False, is_transpose=True)
+            for b, blk in enumerate(blocks):
+                nc.tensor.matmul(den[t][:, blk], pasq[:, blk], ident[:], start=False, stop=b == len(blocks) - 1, is_transpose=True)
+
+        def invert(t):
+            rec[t] = tile("rs%d" % t, [P, S], F32)
+            nc.scalar.activation(rec[t][:], den[t][:], ACT.Abs_reciprocal_sqrt, scale=0.5, bias=0.25)
+            if t < 4:
+                rs = rec[t]
+                rec[t] = tile("rec%d" % t, [P, S], F32)
+                nc.scalar.activation(rec[t][:], rs[:], ACT.Square)
+            if t >= 3:
+                return
+            turned = rec[t]
+            rec[t] = psum.tile([P, S], F32, name="rec_ps%d" % t, tag="bank%d" % t)
+            for b in range(S // P):
+                blk = slice(b * P, (b + 1) * P)
+                nc.tensor.transpose(rec[t][:, blk], turned[:, blk], ident[:])
+
+        def finish(t):
+            nc.vector.tensor_tensor(num[t][:], h[t][:], pa[t][:], ALU.mult)
+            if t >= 4:
+                once = tile("once%d" % t, [P, S], F32)
+                nc.vector.tensor_tensor(once[:], num[t][:], rec[t][:], ALU.mult)
+                nc.vector.tensor_tensor(res[:, t, :], once[:], rec[t][:], ALU.mult)
+            else:
+                nc.vector.tensor_tensor(res[:, t, :], num[t][:], rec[t][:], ALU.mult)
+            nc.sync.dma_start(out_rows[:, t, :], res[:, t, :])
+
+        fetch(0)
+        for t in range(1, PACK):
+            fetch(t)
+            invert(t - 1)
+        invert(PACK - 1)
+        for t in range(PACK):
+            finish(t)
+        res_i = [tile("res_i%d" % c, [P, HALF, PACK], BF16) for c in range(2)]
+        for c in range(2):
+            interleave(res_i[c][:], res[:, :, c * HALF : (c + 1) * HALF])
+        for c in range(2):
+            half = slice(c * HALF, (c + 1) * HALF)
+            nc.vector.quantize_mx(o_c[:, half].bitcast(FP8X4), o_s[:, half], res_i[c][:].rearrange("p c t -> p (c t)"))
+            nc.sync.dma_start(out_words[:, half], o_c[:, half].bitcast(I32))
         for q in range(4):
-            queue = nc.scalar if q % 2 else nc.sync
+            queue = nc.sync if q == 3 else nc.scalar
             queue.dma_start(out_2[0, 4 * q : 4 * q + 4, :].bitcast(I32), o_s[32 * q : 32 * q + 4, :].bitcast(I32))

@@ -66,7 +66,8 @@ def tile_picked_joingatelseharm_none_po_kernel(
             return lst[:, lo // 16 : (lo + n) // 16]
 
         xs_raw = tile("xs_raw", [P, T], U8)
-        nc.vector.memset(xs_raw[:].bitcast(I32), 0)
+        nc.vector.memset(xs_raw[:, : T // 2].bitcast(I32), 0)
+        nc.gpsimd.memset(xs_raw[:, T // 2 :].bitcast(I32), 0)
         w1s_raw = tile("w1s_raw", [P, H], U8)
         nc.gpsimd.memset(w1s_raw[:].bitcast(I32), 0)
         w2s_raw = tile("w2s_raw", [P, N], U8)
@@ -80,28 +81,29 @@ def tile_picked_joingatelseharm_none_po_kernel(
         offs_t = load_list("offs_t", offs)
         w1_raw = tile("w1_raw", [P, 2 * H], U8)
         nc.sync.dma_start(w1_raw[:].bitcast(I32), w1_words[0].bitcast(I32))
-        n1_t = load_list("n1_t", n1)
+        load_scale_rows(nc.sync, xs_raw, x_scales)
+        load_scale_quadrant(nc.sync, w1s_raw, w1_scales, 0)
         xw_raw = tile("xw_raw", [P, T], I32)
         nc.sync.dma_start(xw_raw[:], x_words[0].rearrange("p n t -> p (n t)").bitcast(I32))
-        load_scale_rows(nc.sync, xs_raw, x_scales)
-        for q in range(3):
-            load_scale_quadrant(nc.sync, w1s_raw, w1_scales, q)
-        load_scale_quadrant(nc.gpsimd, w1s_raw, w1_scales, 3)
-        gn_t = tile("gn_t", [P, PACK], F32)
-        nc.gpsimd.dma_start(gn_t[:], gn.rearrange("(p t) o -> p (t o)", t=PACK))
-        gm_t = tile("gm_t", [P, PACK], F32)
-        nc.gpsimd.dma_start(gm_t[:], gm.rearrange("(p t) o -> p (t o)", t=PACK))
+        load_scale_quadrant(nc.sync, w1s_raw, w1_scales, 1)
         ident = tile("ident", [P, P], F32)
+        for q in (2, 3):
+            load_scale_quadrant(nc.gpsimd, w1s_raw, w1_scales, q)
         make_identity(nc, ident[:])
         w2_raw = tile("w2_raw", [P, 2 * N], U8)
         nc.sync.dma_start(w2_raw[:].bitcast(I32), w2_words[0].bitcast(I32))
-        n2_t = load_list("n2_t", n2)
         w3_raw = tile("w3_raw", [P, 2 * N], U8)
         nc.sync.dma_start(w3_raw[:].bitcast(I32), w3_words[0].bitcast(I32))
-        n3_t = load_list("n3_t", n3)
-        n4_t = load_list("n4_t", n4)
         load_scale_rows(nc.sync, w2s_raw, w2_scales)
+        n1_t = load_list("n1_t", n1)
+        gn_t = tile("gn_t", [P, PACK], F32)
+        nc.sync.dma_start(gn_t[:], gn.rearrange("(p t) o -> p (t o)", t=PACK))
+        n2_t = load_list("n2_t", n2)
+        gm_t = tile("gm_t", [P, PACK], F32)
+        nc.sync.dma_start(gm_t[:], gm.rearrange("(p t) o -> p (t o)", t=PACK))
+        n3_t = load_list("n3_t", n3)
         load_scale_rows(nc.sync, w3s_raw, w3_scales)
+        n4_t = load_list("n4_t", n4)
 
         w1_c = deal_words("w1_c", w1_raw)
         xs = [tile("xs%d" % c, [P, HALF], U8) for c in range(2)]
@@ -113,16 +115,19 @@ def tile_picked_joingatelseharm_none_po_kernel(
         def pick_scales(c):
             nc.vector.tensor_copy(xs[c][:], xs_raw[:].indirect(cols(offs_t, c * HALF, HALF)))
 
-        pick_words(0)
         pick_scales(0)
-        w1_s = deal_scales("w1_s", w1s_raw)
-        pick_words(1)
         pick_scales(1)
+        pick_words(0)
+        w1_s = [tile("w1_s%d" % k, [P, n, P], U8) for k, n in enumerate((1, PACK - 1))]
+        w1s_by_tile = w1s_raw[:].rearrange("p (m t) -> p t m", t=PACK)
+        nc.vector.tensor_copy(w1_s[0][:], w1s_by_tile[:, :1, :])
+        pick_words(1)
+        nc.vector.tensor_copy(w1_s[1][:], w1s_by_tile[:, 1:, :])
 
         y_ps = [psum.tile([P, S], F32, name="y_ps%d" % t, tag="bank%d" % t) for t in range(PACK)]
         for c, t in ((0, 0), (1, 0), (0, 1), (1, 1), (0, 2), (1, 2), (0, 3), (1, 3)):
             nc.tensor.matmul_mx(
-                out=y_ps[t][:, c * HALF : (c + 1) * HALF], lhsT=w1_c[:, t, :].bitcast(FP4X4), lhsT_scale=w1_s[:, t, :],
+                out=y_ps[t][:, c * HALF : (c + 1) * HALF], lhsT=w1_c[:, t, :].bitcast(FP4X4), lhsT_scale=w1_s[min(t, 1)][:, max(t - 1, 0), :],
                 rhs=xw[c][:].bitcast(FP8X4), rhs_scale=xs[c][:], start=True, stop=True,
             )
 
@@ -132,15 +137,29 @@ def tile_picked_joingatelseharm_none_po_kernel(
         e2 = [tile("e2_%d" % t, [P, S], F32) for t in range(PACK)]
         sums = tile("sums", [P, PACK, S], F32)
         z_p = tile("z_p", [P, PACK, S], BF16)
-        for t in range(PACK):
-            nc.scalar.activation(th[t][:], y_ps[t][:], ACT.Tanh, scale=0.5)
-            nc.scalar.copy(yex[t][:, :S], y_ps[t][:])
+        def keep_y(t):
+            if t in (3,):
+                nc.vector.tensor_copy(yex[t][:, :S], y_ps[t][:])
+            else:
+                nc.scalar.copy(yex[t][:, :S], y_ps[t][:])
+
+        def gate(t):
             for c in range(2):
                 nc.vector.tensor_scalar(
                     sg[t][:, c * HALF : (c + 1) * HALF], th[t][:].indirect(cols(n1_t, c * HALF, HALF)),
                     0.5, 0.5, ALU.mult, ALU.add,
                 )
+
+        def gated(t):
             nc.vector.scalar_tensor_tensor(z_p[:, t, :], yex[t][:, :S], gn_t[:, t : t + 1], sg[t][:], ALU.mult, ALU.mult)
+
+        for t in range(PACK + 1):
+            if t < PACK:
+                nc.scalar.activation(th[t][:], y_ps[t][:], ACT.Tanh, scale=0.5)
+                gate(t)
+            if t > 0:
+                keep_y(t - 1)
+                gated(t - 1)
         for t in range(PACK):
             nc.scalar.activation(yex[t][:, S:], y_ps[t][:], ACT.Exp)
             nc.scalar.activation(e2[t][:], yex[t][:].indirect(n2_t[:]), ACT.Exp)
@@ -170,11 +189,11 @@ def tile_picked_joingatelseharm_none_po_kernel(
         lse = tile("lse", [P, 2 * PACK, HALF], F32, tag="e2_3")
 
         def log_branch(c, t):
-            dif = tile("dif%d_%d" % (c, t), [P, HALF], F32, tag={(1, 2): "z2_p0", (1, 3): "z2_i0"}.get((c, t)))
+            dif = tile("dif%d_%d" % (c, t), [P, HALF], F32, tag={(1, 2): "dif0_3", (1, 3): "z2_p0"}.get((c, t)))
             nc.vector.tensor_tensor(
                 dif[:], yex[t][:].indirect(cols(n3_t, c * HALF, HALF)), lse[:, PACK * c + t, :], ALU.subtract
             )
-            if PACK * c + t < 6:
+            if PACK * c + t < 7:
                 nc.scalar.activation(z2_p[c][:, t, :], dif[:], ACT.Copy, scale=ngm[:, t : t + 1])
             else:
                 nc.vector.tensor_scalar(z2_p[c][:, t, :], dif[:], ngm[:, t : t + 1], None, ALU.mult)
@@ -206,17 +225,15 @@ def tile_picked_joingatelseharm_none_po_kernel(
         for t in range(2, PACK):
             log_branch(1, t)
         warm = tile("warm", [P, 1], F32)
-        nc.scalar.activation(warm[:], z2_p[1][:, 1, HALF - 1 : HALF], ACT.Abs_reciprocal_sqrt, scale=0.0, bias=1.0)
+        nc.scalar.activation(warm[:], z2_p[1][:, 2, HALF - 1 : HALF], ACT.Abs_reciprocal_sqrt, scale=0.0, bias=1.0)
         second_product(1)
-        h = [tile("h%d" % t, [P, S], F32, tag=("z2_i1", "z2_p1", "dif1_1", "e2_3")[t]) for t in range(PACK)]
+        h = [tile("h%d" % t, [P, S], F32) for t in range(PACK)]
         for t in range(PACK):
             nc.scalar.activation(hsq[:, t, :HALF], h_ps[0][t][:], ACT.Square)
         for t in range(PACK):
             nc.vector.tensor_copy(h[t][:, :HALF], h_ps[0][t][:])
         for t in range(PACK):
             nc.scalar.copy(h[t][:, HALF:], h_ps[1][t][:])
-        for t in range(PACK):
-            nc.scalar.activation(hsq[:, t, HALF:], h_ps[1][t][:], ACT.Square)
 
         o_c = tile("o_c", [P, S], U32)
         o_s = tile("o_s", [P, S], U8)
@@ -226,62 +243,66 @@ def tile_picked_joingatelseharm_none_po_kernel(
         pa = [tile("pa%d" % t, [P, S], F32) for t in range(PACK)]
         num = [tile("num%d" % t, [P, S], F32) for t in range(PACK)]
         den, rec = {}, {}
+        last = PACK - 1
+        blocks = [slice(b * P, (b + 1) * P) for b in range(S // P)]
+        halves = [slice(c * HALF, (c + 1) * HALF) for c in range(2)]
 
         def fetch(t):
+            nc.scalar.activation(hsq[:, t, HALF:], h_ps[1][t][:], ACT.Square)
             for c in range(2):
-                nc.vector.tensor_copy(pa[t][:, c * HALF : (c + 1) * HALF], h[t][:].indirect(cols(n4_t, c * HALF, HALF)))
+                nc.vector.tensor_copy(pa[t][:, halves[c]], h[t][:].indirect(cols(n4_t, c * HALF, HALF)))
             pasq = tile("pasq%d" % t, [P, S], F32)
             nc.scalar.activation(pasq[:], pa[t][:], ACT.Square)
-            if t >= 3:
-                den[t] = tile("den%d" % t, [P, S], F32)
+            if t == last:
+                den[t] = tile("den", [P, S], F32)
                 nc.vector.tensor_tensor(den[t][:], hsq[:, t, :], pasq[:], ALU.add)
                 return
             den[t] = psum.tile([P, S], F32, name="den_ps%d" % t, tag="bank%d" % (PACK + t))
-            blocks = [slice(b * P, (b + 1) * P) for b in range(S // P)]
             for b, blk in enumerate(blocks):
                 nc.tensor.matmul(den[t][:, blk], hsq[:, t, blk], ident[:], start=b == 0, stop=False, is_transpose=True)
             for b, blk in enumerate(blocks):
                 nc.tensor.matmul(den[t][:, blk], pasq[:, blk], ident[:], start=False, stop=b == len(blocks) - 1, is_transpose=True)
 
         def invert(t):
-            rec[t] = tile("rs%d" % t, [P, S], F32)
-            nc.scalar.activation(rec[t][:], den[t][:], ACT.Abs_reciprocal_sqrt, scale=0.5, bias=0.25)
-            if t < 4:
-                rs = rec[t]
-                rec[t] = tile("rec%d" % t, [P, S], F32)
-                nc.scalar.activation(rec[t][:], rs[:], ACT.Square)
-            if t >= 3:
+            rs = tile("rs%d" % t, [P, S], F32)
+            rec[t] = tile("rec%d" % t, [P, S], F32)
+            for part in halves if t == last else [slice(0, S)]:
+                nc.scalar.activation(rs[:, part], den[t][:, part], ACT.Abs_reciprocal_sqrt, scale=0.5, bias=0.25)
+                nc.scalar.activation(rec[t][:, part], rs[:, part], ACT.Square)
+            if t == last:
                 return
             turned = rec[t]
             rec[t] = psum.tile([P, S], F32, name="rec_ps%d" % t, tag="bank%d" % t)
-            for b in range(S // P):
-                blk = slice(b * P, (b + 1) * P)
+            for blk in blocks:
                 nc.tensor.transpose(rec[t][:, blk], turned[:, blk], ident[:])
 
-        def finish(t):
+        def product(t):
             nc.vector.tensor_tensor(num[t][:], h[t][:], pa[t][:], ALU.mult)
-            if t >= 4:
-                once = tile("once%d" % t, [P, S], F32)
-                nc.vector.tensor_tensor(once[:], num[t][:], rec[t][:], ALU.mult)
-                nc.vector.tensor_tensor(res[:, t, :], once[:], rec[t][:], ALU.mult)
-            else:
-                nc.vector.tensor_tensor(res[:, t, :], num[t][:], rec[t][:], ALU.mult)
-            nc.sync.dma_start(out_rows[:, t, :], res[:, t, :])
+
+        def finish(t, part):
+            nc.vector.tensor_tensor(res[:, t, part], num[t][:, part], rec[t][:, part], ALU.mult)
+            nc.sync.dma_start(out_rows[:, t, part], res[:, t, part])
+
+        res_i = [tile("res_i%d" % c, [P, HALF, PACK], BF16) for c in range(2)]
+
+        def planes(c):
+            nc.vector.quantize_mx(o_c[:, halves[c]].bitcast(FP8X4), o_s[:, halves[c]], res_i[c][:].rearrange("p c t -> p (c t)"))
+            nc.sync.dma_start(out_words[:, halves[c]], o_c[:, halves[c]].bitcast(I32))
 
         fetch(0)
         for t in range(1, PACK):
             fetch(t)
             invert(t - 1)
-        invert(PACK - 1)
+        invert(last)
         for t in range(PACK):
-            finish(t)
-        res_i = [tile("res_i%d" % c, [P, HALF, PACK], BF16) for c in range(2)]
+            product(t)
+        for t in range(last):
+            finish(t, slice(0, S))
         for c in range(2):
-            interleave(res_i[c][:], res[:, :, c * HALF : (c + 1) * HALF])
+            finish(last, halves[c])
+            interleave(res_i[c][:], res[:, :, halves[c]])
         for c in range(2):
-            half = slice(c * HALF, (c + 1) * HALF)
-            nc.vector.quantize_mx(o_c[:, half].bitcast(FP8X4), o_s[:, half], res_i[c][:].rearrange("p c t -> p (c t)"))
-            nc.sync.dma_start(out_words[:, half], o_c[:, half].bitcast(I32))
+            planes(c)
         for q in range(4):
             queue = nc.sync if q == 3 else nc.scalar
             queue.dma_start(out_2[0, 4 * q : 4 * q + 4, :].bitcast(I32), o_s[32 * q : 32 * q + 4, :].bitcast(I32))

@@ -4,7 +4,7 @@ import concourse.mybir as mybir
 from concourse.masks import make_identity
 
 K, T, S, N, H = 512, 2048, 512, 512, 512
-FLOPS = 3 * 2 * 512 * 512 * 512
+FLOPS = 2 * S * (K * H + 2 * H * N)
 
 F32 = mybir.dt.float32
 BF16 = mybir.dt.bfloat16
@@ -18,8 +18,14 @@ ALU = mybir.AluOpType
 ACT = mybir.ActivationFunctionType
 
 P = 128
-PACK = 4
+TILES = 4
+LAST = TILES - 1
+QUADRANTS = 4
 HALF = S // 2
+HALVES = [slice(0, HALF), slice(HALF, S)]
+BLOCKS = [slice(b * P, (b + 1) * P) for b in range(S // P)]
+WHOLE = slice(0, S)
+SUMMED_ON_TENSOR = 2
 
 
 def tile_picked_joingatelseharm_none_po_kernel(
@@ -31,278 +37,264 @@ def tile_picked_joingatelseharm_none_po_kernel(
         keep = ctx.enter_context(tc.tile_pool(name="keep", bufs=1))
         psum = ctx.enter_context(tc.psum_pool(name="psum", bufs=1))
 
-        def tile(name, shape, dtype, tag=None):
-            return keep.tile(shape, dtype, name=name, tag=tag or name, align_bytes=64)
+        def tile(name, shape, dtype, after=None):
+            return keep.tile(shape, dtype, name=name, tag=after or name, align_bytes=64)
+
+        def bank(name, number, width):
+            return psum.tile([P, width], F32, name=name, tag="bank%d" % number)
 
         def load_list(name, src):
-            lst = keep.tile([P, S // 16], U16, name=name)
-            nc.sync.dma_start(lst[:], src)
-            return lst
+            offsets = keep.tile([P, S // 16], U16, name=name)
+            nc.sync.dma_start(offsets[:], src)
+            return offsets
 
-        def load_scale_rows(queue, dst, src):
-            for q in range(4):
-                queue.dma_start(dst[32 * q : 32 * q + 4, :].bitcast(I32), src[0, 4 * q : 4 * q + 4, :].bitcast(I32))
+        def entries(offsets, c):
+            return offsets[:, c * HALF // 16 : (c + 1) * HALF // 16]
 
-        def deal_words(name, raw):
-            dealt = tile(name, [P, PACK, 2 * P], U8)
+        def scale_plane(name, width):
+            plane = tile(name, [P, width], U8)
+            nc.vector.memset(plane[:].bitcast(I32), 0)
+            return plane
+
+        def load_scale_rows(plane, src, quadrants):
+            for q in quadrants:
+                nc.sync.dma_start(plane[32 * q : 32 * q + 4, :].bitcast(I32), src[0, 4 * q : 4 * q + 4, :].bitcast(I32))
+
+        def load_words(name, src):
+            words = tile(name, [P, src.shape[2]], U8)
+            nc.sync.dma_start(words[:].bitcast(I32), src[0].bitcast(I32))
+            return words
+
+        def load_gain(name, src):
+            gain = tile(name, [P, TILES], F32)
+            nc.sync.dma_start(gain[:], src.rearrange("(p t) o -> p (t o)", t=TILES))
+            return gain
+
+        def deal_words(name, words):
+            dealt = tile(name, [P, TILES, 2 * P], U8)
             nc.vector.tensor_copy(
-                dealt[:].rearrange("p t (m b) -> p m t b", b=2),
-                raw[:].rearrange("p (m t b) -> p m t b", t=PACK, b=2),
+                dealt[:].rearrange("p t (m b) -> p t m b", b=2),
+                words[:].rearrange("p (m t b) -> p t m b", t=TILES, b=2),
             )
             return dealt
 
-        def deal_scales(name, raw):
-            dealt = tile(name, [P, PACK, P], U8)
-            nc.vector.tensor_copy(dealt[:], raw[:].rearrange("p (m t) -> p t m", t=PACK))
+        def deal_scales(name, plane, tiles):
+            dealt = tile(name, [P, len(tiles), P], U8)
+            by_tile = plane[:].rearrange("p (m t) -> p t m", t=TILES)
+            nc.vector.tensor_copy(dealt[:], by_tile[:, tiles.start : tiles.stop, :])
             return dealt
 
-        def interleave(dst, src):
-            nc.vector.tensor_copy(
-                dst.rearrange("p (c i) t -> p c t i", i=4),
-                src.rearrange("p t (c i) -> p c t i", i=4),
-            )
+        def interleave(copy, dst, src):
+            copy(dst.rearrange("p (c i) t -> p c t i", i=4), src.rearrange("p t (c i) -> p c t i", i=4))
 
-        def cols(lst, lo, n):
-            return lst[:, lo // 16 : (lo + n) // 16]
+        def quantise(codes, scales, interleaved):
+            nc.vector.quantize_mx(codes.bitcast(FP8X4), scales, interleaved.rearrange("p c t -> p (c t)"))
 
-        xs_raw = tile("xs_raw", [P, T], U8)
-        nc.vector.memset(xs_raw[:, : T // 2].bitcast(I32), 0)
-        nc.gpsimd.memset(xs_raw[:, T // 2 :].bitcast(I32), 0)
-        w1s_raw = tile("w1s_raw", [P, H], U8)
-        nc.gpsimd.memset(w1s_raw[:].bitcast(I32), 0)
-        w2s_raw = tile("w2s_raw", [P, N], U8)
-        nc.vector.memset(w2s_raw[:].bitcast(I32), 0)
-        w3s_raw = tile("w3s_raw", [P, N], U8)
-        nc.vector.memset(w3s_raw[:].bitcast(I32), 0)
-
-        def load_scale_quadrant(queue, dst, src, q):
-            queue.dma_start(dst[32 * q : 32 * q + 4, :].bitcast(I32), src[0, 4 * q : 4 * q + 4, :].bitcast(I32))
-
+        xs_plane = scale_plane("xs_plane", T)
+        w1s_plane = scale_plane("w1s_plane", H)
+        w2s_plane = scale_plane("w2s_plane", N)
+        w3s_plane = scale_plane("w3s_plane", N)
         offs_t = load_list("offs_t", offs)
-        w1_raw = tile("w1_raw", [P, 2 * H], U8)
-        nc.sync.dma_start(w1_raw[:].bitcast(I32), w1_words[0].bitcast(I32))
-        load_scale_rows(nc.sync, xs_raw, x_scales)
-        load_scale_quadrant(nc.sync, w1s_raw, w1_scales, 0)
-        xw_raw = tile("xw_raw", [P, T], I32)
-        nc.sync.dma_start(xw_raw[:], x_words[0].rearrange("p n t -> p (n t)").bitcast(I32))
-        load_scale_quadrant(nc.sync, w1s_raw, w1_scales, 1)
-        ident = tile("ident", [P, P], F32)
-        for q in (2, 3):
-            load_scale_quadrant(nc.gpsimd, w1s_raw, w1_scales, q)
-        make_identity(nc, ident[:])
-        w2_raw = tile("w2_raw", [P, 2 * N], U8)
-        nc.sync.dma_start(w2_raw[:].bitcast(I32), w2_words[0].bitcast(I32))
-        w3_raw = tile("w3_raw", [P, 2 * N], U8)
-        nc.sync.dma_start(w3_raw[:].bitcast(I32), w3_words[0].bitcast(I32))
-        load_scale_rows(nc.sync, w2s_raw, w2_scales)
+        w1_raw = load_words("w1_raw", w1_words)
+        load_scale_rows(xs_plane, x_scales, range(QUADRANTS))
+        load_scale_rows(w1s_plane, w1_scales, range(1))
+        xw_table = tile("xw_table", [P, T], I32)
+        nc.sync.dma_start(xw_table[:], x_words[0].rearrange("p n r -> p (n r)").bitcast(I32))
+        load_scale_rows(w1s_plane, w1_scales, range(1, QUADRANTS))
+        identity = tile("identity", [P, P], F32)
+        make_identity(nc, identity[:])
+        w2_raw = load_words("w2_raw", w2_words)
+        w3_raw = load_words("w3_raw", w3_words)
+        load_scale_rows(w2s_plane, w2_scales, range(QUADRANTS))
         n1_t = load_list("n1_t", n1)
-        gn_t = tile("gn_t", [P, PACK], F32)
-        nc.sync.dma_start(gn_t[:], gn.rearrange("(p t) o -> p (t o)", t=PACK))
+        gn_t = load_gain("gn_t", gn)
         n2_t = load_list("n2_t", n2)
-        gm_t = tile("gm_t", [P, PACK], F32)
-        nc.sync.dma_start(gm_t[:], gm.rearrange("(p t) o -> p (t o)", t=PACK))
+        gm_t = load_gain("gm_t", gm)
         n3_t = load_list("n3_t", n3)
-        load_scale_rows(nc.sync, w3s_raw, w3_scales)
+        load_scale_rows(w3s_plane, w3_scales, range(QUADRANTS))
         n4_t = load_list("n4_t", n4)
 
         w1_c = deal_words("w1_c", w1_raw)
         xs = [tile("xs%d" % c, [P, HALF], U8) for c in range(2)]
         xw = [tile("xw%d" % c, [P, HALF], U32) for c in range(2)]
+        for c in range(2):
+            nc.vector.tensor_copy(xs[c][:], xs_plane[:].indirect(entries(offs_t, c)))
+        nc.vector.tensor_copy(xw[0][:], xw_table[:].bitcast(U32).indirect(entries(offs_t, 0)))
+        w1s_first = deal_scales("w1s_first", w1s_plane, range(1))
+        nc.vector.tensor_copy(xw[1][:], xw_table[:].bitcast(U32).indirect(entries(offs_t, 1)))
+        w1s_rest = deal_scales("w1s_rest", w1s_plane, range(1, TILES))
+        w1_s = [w1s_first[:, 0, :]] + [w1s_rest[:, t, :] for t in range(LAST)]
 
-        def pick_words(c):
-            nc.vector.tensor_copy(xw[c][:], xw_raw[:].bitcast(U32).indirect(cols(offs_t, c * HALF, HALF)))
-
-        def pick_scales(c):
-            nc.vector.tensor_copy(xs[c][:], xs_raw[:].indirect(cols(offs_t, c * HALF, HALF)))
-
-        pick_scales(0)
-        pick_scales(1)
-        pick_words(0)
-        w1_s = [tile("w1_s%d" % k, [P, n, P], U8) for k, n in enumerate((1, PACK - 1))]
-        w1s_by_tile = w1s_raw[:].rearrange("p (m t) -> p t m", t=PACK)
-        nc.vector.tensor_copy(w1_s[0][:], w1s_by_tile[:, :1, :])
-        pick_words(1)
-        nc.vector.tensor_copy(w1_s[1][:], w1s_by_tile[:, 1:, :])
-
-        y_ps = [psum.tile([P, S], F32, name="y_ps%d" % t, tag="bank%d" % t) for t in range(PACK)]
-        for c, t in ((0, 0), (1, 0), (0, 1), (1, 1), (0, 2), (1, 2), (0, 3), (1, 3)):
-            nc.tensor.matmul_mx(
-                out=y_ps[t][:, c * HALF : (c + 1) * HALF], lhsT=w1_c[:, t, :].bitcast(FP4X4), lhsT_scale=w1_s[min(t, 1)][:, max(t - 1, 0), :],
-                rhs=xw[c][:].bitcast(FP8X4), rhs_scale=xs[c][:], start=True, stop=True,
-            )
-
-        th = [tile("th%d" % t, [P, S], F32) for t in range(PACK)]
-        yex = [tile("yex%d" % t, [P, 2 * S], F32) for t in range(PACK)]
-        sg = [tile("sg%d" % t, [P, S], F32) for t in range(PACK)]
-        e2 = [tile("e2_%d" % t, [P, S], F32) for t in range(PACK)]
-        sums = tile("sums", [P, PACK, S], F32)
-        z_p = tile("z_p", [P, PACK, S], BF16)
-        def keep_y(t):
-            if t in (3,):
-                nc.vector.tensor_copy(yex[t][:, :S], y_ps[t][:])
-            else:
-                nc.scalar.copy(yex[t][:, :S], y_ps[t][:])
-
-        def gate(t):
+        y_ps = [bank("y_ps%d" % t, t, S) for t in range(TILES)]
+        for t in range(TILES):
             for c in range(2):
-                nc.vector.tensor_scalar(
-                    sg[t][:, c * HALF : (c + 1) * HALF], th[t][:].indirect(cols(n1_t, c * HALF, HALF)),
-                    0.5, 0.5, ALU.mult, ALU.add,
+                nc.tensor.matmul_mx(
+                    out=y_ps[t][:, HALVES[c]], lhsT=w1_c[:, t, :].bitcast(FP4X4), lhsT_scale=w1_s[t],
+                    rhs=xw[c][:].bitcast(FP8X4), rhs_scale=xs[c][:], start=True, stop=True,
                 )
 
-        def gated(t):
-            nc.vector.scalar_tensor_tensor(z_p[:, t, :], yex[t][:, :S], gn_t[:, t : t + 1], sg[t][:], ALU.mult, ALU.mult)
+        tanh_y = [tile("tanh_y%d" % t, [P, S], F32) for t in range(TILES)]
+        y_ex = [tile("y_ex%d" % t, [P, 2 * S], F32) for t in range(TILES)]
+        gate = [tile("gate%d" % t, [P, S], F32) for t in range(TILES)]
+        ex_n2 = [tile("ex_n2_%d" % t, [P, S], F32) for t in range(TILES)]
+        ex_sum = tile("ex_sum", [P, TILES, S], F32)
+        z_tiles = tile("z_tiles", [P, TILES, S], BF16)
 
-        for t in range(PACK + 1):
-            if t < PACK:
-                nc.scalar.activation(th[t][:], y_ps[t][:], ACT.Tanh, scale=0.5)
-                gate(t)
-            if t > 0:
-                keep_y(t - 1)
-                gated(t - 1)
-        for t in range(PACK):
-            nc.scalar.activation(yex[t][:, S:], y_ps[t][:], ACT.Exp)
-            nc.scalar.activation(e2[t][:], yex[t][:].indirect(n2_t[:]), ACT.Exp)
-            nc.vector.tensor_tensor(sums[:, t, :], yex[t][:, S:], e2[t][:], ALU.add)
+        def fetch_gate(t):
+            nc.scalar.activation(tanh_y[t][:], y_ps[t][:], ACT.Tanh, scale=0.5)
+            for c in range(2):
+                nc.vector.tensor_scalar(
+                    gate[t][:, HALVES[c]], tanh_y[t][:].indirect(entries(n1_t, c)), 0.5, 0.5, ALU.mult, ALU.add
+                )
 
-        ngm = tile("ngm", [P, PACK], F32)
-        nc.scalar.activation(ngm[:], gm_t[:], ACT.Copy, scale=-1.0)
+        def apply_gate(t):
+            copy = nc.vector.tensor_copy if t == LAST else nc.scalar.copy
+            copy(y_ex[t][:, :S], y_ps[t][:])
+            nc.vector.scalar_tensor_tensor(z_tiles[:, t, :], y_ex[t][:, :S], gn_t[:, t : t + 1], gate[t][:], ALU.mult, ALU.mult)
+
+        fetch_gate(0)
+        for t in range(1, TILES):
+            fetch_gate(t)
+            apply_gate(t - 1)
+        apply_gate(LAST)
+
+        for t in range(TILES):
+            nc.scalar.activation(y_ex[t][:, S:], y_ps[t][:], ACT.Exp)
+            nc.scalar.activation(ex_n2[t][:], y_ex[t][:].indirect(n2_t[:]), ACT.Exp)
+            nc.vector.tensor_tensor(ex_sum[:, t, :], y_ex[t][:, S:], ex_n2[t][:], ALU.add)
+
+        minus_gm = tile("minus_gm", [P, TILES], F32)
+        nc.scalar.activation(minus_gm[:], gm_t[:], ACT.Copy, scale=-1.0)
         w2_c = deal_words("w2_c", w2_raw)
         w3_c = deal_words("w3_c", w3_raw)
-        z_i = tile("z_i", [P, S, PACK], BF16)
-        interleave(z_i[:], z_p[:])
-        w2_s = deal_scales("w2_s", w2s_raw)
+        z_woven = tile("z_woven", [P, S, TILES], BF16)
+        interleave(nc.vector.tensor_copy, z_woven[:], z_tiles[:])
+        w2_s = deal_scales("w2_s", w2s_plane, range(TILES))
         z_c = tile("z_c", [P, S], U32)
         z_s = tile("z_s", [P, S], U8)
-        nc.vector.quantize_mx(z_c[:].bitcast(FP8X4), z_s[:], z_i[:].rearrange("p c t -> p (c t)"))
-        w3_s = deal_scales("w3_s", w3s_raw)
+        quantise(z_c[:], z_s[:], z_woven[:])
+        w3_s = deal_scales("w3_s", w3s_plane, range(TILES))
 
         z2_c = [tile("z2_c%d" % c, [P, HALF], U32) for c in range(2)]
         z2_s = [tile("z2_s%d" % c, [P, HALF], U8) for c in range(2)]
-        z2_p = [tile("z2_p%d" % c, [P, PACK, HALF], BF16) for c in range(2)]
-        z2_i = [tile("z2_i%d" % c, [P, HALF, PACK], BF16) for c in range(2)]
-        h_ps = [
-            [psum.tile([P, HALF], F32, name="h_ps%d_%d" % (c, t), tag="bank%d" % (PACK * (1 - c) + t)) for t in range(PACK)]
-            for c in range(2)
-        ]
-        hsq = tile("hsq", [P, PACK, S], F32)
-        lse = tile("lse", [P, 2 * PACK, HALF], F32, tag="e2_3")
+        z2_tiles = [tile("z2_tiles%d" % c, [P, TILES, HALF], BF16) for c in range(2)]
+        z2_woven = [tile("z2_woven%d" % c, [P, HALF, TILES], BF16) for c in range(2)]
+        h_ps = [[bank("h_ps%d_%d" % (c, t), TILES * (1 - c) + t, HALF) for t in range(TILES)] for c in range(2)]
+        h_sq = tile("h_sq", [P, TILES, S], F32)
+        log_sum = tile("log_sum", [P, 2 * TILES, HALF], F32, after="ex_n2_%d" % LAST)
+        taken_over = {(1, LAST - 1): "diff0_%d" % LAST, (1, LAST): "z2_tiles0"}
 
-        def log_branch(c, t):
-            dif = tile("dif%d_%d" % (c, t), [P, HALF], F32, tag={(1, 2): "dif0_3", (1, 3): "z2_p0"}.get((c, t)))
-            nc.vector.tensor_tensor(
-                dif[:], yex[t][:].indirect(cols(n3_t, c * HALF, HALF)), lse[:, PACK * c + t, :], ALU.subtract
-            )
-            if PACK * c + t < 7:
-                nc.scalar.activation(z2_p[c][:, t, :], dif[:], ACT.Copy, scale=ngm[:, t : t + 1])
+        def make_z2(c, t):
+            diff = tile("diff%d_%d" % (c, t), [P, HALF], F32, after=taken_over.get((c, t)))
+            nc.vector.tensor_tensor(diff[:], y_ex[t][:].indirect(entries(n3_t, c)), log_sum[:, TILES * c + t, :], ALU.subtract)
+            if (c, t) == (1, LAST):
+                nc.vector.tensor_scalar(z2_tiles[c][:, t, :], diff[:], minus_gm[:, t : t + 1], None, ALU.mult)
             else:
-                nc.vector.tensor_scalar(z2_p[c][:, t, :], dif[:], ngm[:, t : t + 1], None, ALU.mult)
+                nc.scalar.activation(z2_tiles[c][:, t, :], diff[:], ACT.Copy, scale=minus_gm[:, t : t + 1])
 
-        def second_product(c):
-            interleave(z2_i[c][:], z2_p[c][:])
-            nc.vector.quantize_mx(z2_c[c][:].bitcast(FP8X4), z2_s[c][:], z2_i[c][:].rearrange("p c t -> p (c t)"))
-            for t in range(PACK):
+        def make_h(c):
+            interleave(nc.vector.tensor_copy, z2_woven[c][:], z2_tiles[c][:])
+            quantise(z2_c[c][:], z2_s[c][:], z2_woven[c][:])
+            for t in range(TILES):
                 for b in range(HALF // P):
-                    inner = slice(b * P, (b + 1) * P)
-                    outer = slice(c * HALF + b * P, c * HALF + (b + 1) * P)
+                    in_half, in_all = BLOCKS[b], BLOCKS[HALF // P * c + b]
                     nc.tensor.matmul_mx(
-                        out=h_ps[c][t][:, inner], lhsT=w2_c[:, t, :].bitcast(FP4X4), lhsT_scale=w2_s[:, t, :],
-                        rhs=z_c[:, outer].bitcast(FP8X4), rhs_scale=z_s[:, outer], start=True, stop=False,
+                        out=h_ps[c][t][:, in_half], lhsT=w2_c[:, t, :].bitcast(FP4X4), lhsT_scale=w2_s[:, t, :],
+                        rhs=z_c[:, in_all].bitcast(FP8X4), rhs_scale=z_s[:, in_all], start=True, stop=False,
                     )
                     nc.tensor.matmul_mx(
-                        out=h_ps[c][t][:, inner], lhsT=w3_c[:, t, :].bitcast(FP4X4), lhsT_scale=w3_s[:, t, :],
-                        rhs=z2_c[c][:, inner].bitcast(FP8X4), rhs_scale=z2_s[c][:, inner], start=False, stop=True,
+                        out=h_ps[c][t][:, in_half], lhsT=w3_c[:, t, :].bitcast(FP4X4), lhsT_scale=w3_s[:, t, :],
+                        rhs=z2_c[c][:, in_half].bitcast(FP8X4), rhs_scale=z2_s[c][:, in_half], start=False, stop=True,
                     )
 
         for c in range(2):
-            for t in range(PACK):
-                nc.scalar.activation(lse[:, PACK * c + t, :], sums[:, t, c * HALF : (c + 1) * HALF], ACT.Ln)
-        for t in range(PACK):
-            log_branch(0, t)
-        for t in range(2):
-            log_branch(1, t)
-        second_product(0)
-        for t in range(2, PACK):
-            log_branch(1, t)
-        warm = tile("warm", [P, 1], F32)
-        nc.scalar.activation(warm[:], z2_p[1][:, 2, HALF - 1 : HALF], ACT.Abs_reciprocal_sqrt, scale=0.0, bias=1.0)
-        second_product(1)
-        h = [tile("h%d" % t, [P, S], F32) for t in range(PACK)]
-        for t in range(PACK):
-            nc.scalar.activation(hsq[:, t, :HALF], h_ps[0][t][:], ACT.Square)
-        for t in range(PACK):
-            nc.vector.tensor_copy(h[t][:, :HALF], h_ps[0][t][:])
-        for t in range(PACK):
-            nc.scalar.copy(h[t][:, HALF:], h_ps[1][t][:])
+            for t in range(TILES):
+                nc.scalar.activation(log_sum[:, TILES * c + t, :], ex_sum[:, t, HALVES[c]], ACT.Ln)
+        for t in range(TILES):
+            make_z2(0, t)
+        for t in range(LAST - 1):
+            make_z2(1, t)
+        make_h(0)
+        for t in range(LAST - 1, TILES):
+            make_z2(1, t)
+        sixteen = tile("sixteen", [P, 1], F32)
+        nc.vector.memset(sixteen[:], 16.0)
+        quarter = tile("quarter", [P, 1], F32, after=taken_over[(1, LAST - 1)])
+        nc.scalar.activation(quarter[:], sixteen[:], ACT.Abs_reciprocal_sqrt)
+        make_h(1)
 
-        o_c = tile("o_c", [P, S], U32)
-        o_s = tile("o_s", [P, S], U8)
-        out_rows = out_0.rearrange("(p t) c -> p t c", t=PACK)
-        out_words = out_1[0].rearrange("p n t -> p (n t)").bitcast(I32)
-        res = tile("res", [P, PACK, S], F32)
-        pa = [tile("pa%d" % t, [P, S], F32) for t in range(PACK)]
-        num = [tile("num%d" % t, [P, S], F32) for t in range(PACK)]
-        den, rec = {}, {}
-        last = PACK - 1
-        blocks = [slice(b * P, (b + 1) * P) for b in range(S // P)]
-        halves = [slice(c * HALF, (c + 1) * HALF) for c in range(2)]
+        h = [tile("h%d" % t, [P, S], F32) for t in range(TILES)]
+        for t in range(TILES):
+            nc.scalar.activation(h_sq[:, t, HALVES[0]], h_ps[0][t][:], ACT.Square)
+        for t in range(TILES):
+            nc.vector.tensor_copy(h[t][:, HALVES[0]], h_ps[0][t][:])
+        for t in range(TILES):
+            nc.scalar.copy(h[t][:, HALVES[1]], h_ps[1][t][:])
 
-        def fetch(t):
-            nc.scalar.activation(hsq[:, t, HALF:], h_ps[1][t][:], ACT.Square)
+        out_c = tile("out_c", [P, S], U32)
+        out_s = tile("out_s", [P, S], U8)
+        out_rows = out_0.rearrange("(p t) c -> p t c", t=TILES)
+        out_words = out_1[0].rearrange("p n r -> p (n r)").bitcast(I32)
+        result = tile("result", [P, TILES, S], F32)
+        pa = [tile("pa%d" % t, [P, S], F32) for t in range(TILES)]
+        squares, factor, product = {}, {}, {}
+
+        def fetch_pa(t):
+            nc.scalar.activation(h_sq[:, t, HALVES[1]], h_ps[1][t][:], ACT.Square)
             for c in range(2):
-                nc.vector.tensor_copy(pa[t][:, halves[c]], h[t][:].indirect(cols(n4_t, c * HALF, HALF)))
-            pasq = tile("pasq%d" % t, [P, S], F32)
-            nc.scalar.activation(pasq[:], pa[t][:], ACT.Square)
-            if t == last:
-                den[t] = tile("den", [P, S], F32)
-                nc.vector.tensor_tensor(den[t][:], hsq[:, t, :], pasq[:], ALU.add)
+                nc.vector.tensor_copy(pa[t][:, HALVES[c]], h[t][:].indirect(entries(n4_t, c)))
+            pa_sq = tile("pa_sq%d" % t, [P, S], F32)
+            nc.scalar.activation(pa_sq[:], pa[t][:], ACT.Square)
+            if t >= SUMMED_ON_TENSOR:
+                squares[t] = tile("squares%d" % t, [P, S], F32)
+                nc.vector.tensor_tensor(squares[t][:], h_sq[:, t, :], pa_sq[:], ALU.add)
                 return
-            den[t] = psum.tile([P, S], F32, name="den_ps%d" % t, tag="bank%d" % (PACK + t))
-            for b, blk in enumerate(blocks):
-                nc.tensor.matmul(den[t][:, blk], hsq[:, t, blk], ident[:], start=b == 0, stop=False, is_transpose=True)
-            for b, blk in enumerate(blocks):
-                nc.tensor.matmul(den[t][:, blk], pasq[:, blk], ident[:], start=False, stop=b == len(blocks) - 1, is_transpose=True)
+            squares[t] = bank("squares_ps%d" % t, TILES + t, S)
+            for blk in BLOCKS:
+                nc.tensor.matmul(
+                    squares[t][:, blk], h_sq[:, t, blk], identity[:], start=blk == BLOCKS[0], stop=False, is_transpose=True
+                )
+            for blk in BLOCKS:
+                nc.tensor.matmul(
+                    squares[t][:, blk], pa_sq[:, blk], identity[:], start=False, stop=blk == BLOCKS[-1], is_transpose=True
+                )
 
         def invert(t):
-            rs = tile("rs%d" % t, [P, S], F32)
-            rec[t] = tile("rec%d" % t, [P, S], F32)
-            for part in halves if t == last else [slice(0, S)]:
-                nc.scalar.activation(rs[:, part], den[t][:, part], ACT.Abs_reciprocal_sqrt, scale=0.5, bias=0.25)
-                nc.scalar.activation(rec[t][:, part], rs[:, part], ACT.Square)
-            if t == last:
-                return
-            turned = rec[t]
-            rec[t] = psum.tile([P, S], F32, name="rec_ps%d" % t, tag="bank%d" % t)
-            for blk in blocks:
-                nc.tensor.transpose(rec[t][:, blk], turned[:, blk], ident[:])
-
-        def product(t):
-            nc.vector.tensor_tensor(num[t][:], h[t][:], pa[t][:], ALU.mult)
+            root = tile("root%d" % t, [P, S], F32)
+            factor[t] = tile("factor%d" % t, [P, S], F32)
+            for part in HALVES if t >= SUMMED_ON_TENSOR else [WHOLE]:
+                nc.scalar.activation(root[:, part], squares[t][:, part], ACT.Abs_reciprocal_sqrt, scale=0.5, bias=quarter[:])
+                nc.scalar.activation(factor[t][:, part], root[:, part], ACT.Square)
+            if t < SUMMED_ON_TENSOR:
+                transposed = factor[t]
+                factor[t] = bank("factor_ps%d" % t, t, S)
+                for blk in BLOCKS:
+                    nc.tensor.transpose(factor[t][:, blk], transposed[:, blk], identity[:])
 
         def finish(t, part):
-            nc.vector.tensor_tensor(res[:, t, part], num[t][:, part], rec[t][:, part], ALU.mult)
-            nc.sync.dma_start(out_rows[:, t, part], res[:, t, part])
+            nc.vector.tensor_tensor(result[:, t, part], product[t][:, part], factor[t][:, part], ALU.mult)
+            nc.sync.dma_start(out_rows[:, t, part], result[:, t, part])
 
-        res_i = [tile("res_i%d" % c, [P, HALF, PACK], BF16) for c in range(2)]
-
-        def planes(c):
-            nc.vector.quantize_mx(o_c[:, halves[c]].bitcast(FP8X4), o_s[:, halves[c]], res_i[c][:].rearrange("p c t -> p (c t)"))
-            nc.sync.dma_start(out_words[:, halves[c]], o_c[:, halves[c]].bitcast(I32))
-
-        fetch(0)
-        for t in range(1, PACK):
-            fetch(t)
+        fetch_pa(0)
+        for t in range(1, TILES):
+            fetch_pa(t)
             invert(t - 1)
-        invert(last)
-        for t in range(PACK):
-            product(t)
-        for t in range(last):
-            finish(t, slice(0, S))
+        invert(LAST)
+        for t in range(TILES):
+            product[t] = tile("product%d" % t, [P, S], F32, after="pa_sq%d" % t)
+            nc.vector.tensor_tensor(product[t][:], h[t][:], pa[t][:], ALU.mult)
+        for t in range(LAST):
+            finish(t, WHOLE)
+        for part in HALVES:
+            finish(LAST, part)
+
+        woven = [tile("woven%d" % c, [P, HALF, TILES], BF16) for c in range(2)]
+        interleave(nc.vector.tensor_copy, woven[0][:], result[:, :, HALVES[0]])
+        interleave(nc.vector.tensor_copy, woven[1][:, :P, :], result[:, :, BLOCKS[-2]])
+        interleave(nc.scalar.copy, woven[1][:, P:, :], result[:, :, BLOCKS[-1]])
         for c in range(2):
-            finish(last, halves[c])
-            interleave(res_i[c][:], res[:, :, halves[c]])
-        for c in range(2):
-            planes(c)
-        for q in range(4):
-            queue = nc.sync if q == 3 else nc.scalar
-            queue.dma_start(out_2[0, 4 * q : 4 * q + 4, :].bitcast(I32), o_s[32 * q : 32 * q + 4, :].bitcast(I32))
+            quantise(out_c[:, HALVES[c]], out_s[:, HALVES[c]], woven[c][:])
+            nc.sync.dma_start(out_words[:, HALVES[c]], out_c[:, HALVES[c]].bitcast(I32))
+        for q in range(QUADRANTS):
+            queue = nc.sync if q == QUADRANTS - 1 else nc.scalar
+            queue.dma_start(out_2[0, 4 * q : 4 * q + 4, :].bitcast(I32), out_s[32 * q : 32 * q + 4, :].bitcast(I32))

from contextlib import ExitStack

import concourse.mybir as mybir
from concourse.masks import make_identity

K, T, S, N, H = 512, 2048, 512, 512, 512
FLOPS = 2 * S * (K * H + 2 * H * N)

F32 = mybir.dt.float32
BF16 = mybir.dt.bfloat16
I32 = mybir.dt.int32
U32 = mybir.dt.uint32
U16 = mybir.dt.uint16
U8 = mybir.dt.uint8
FP8X4 = mybir.dt.float8_e4m3fn_x4
FP4X4 = mybir.dt.float4_e2m1fn_x4
ALU = mybir.AluOpType
ACT = mybir.ActivationFunctionType

P = 128
TILES = 4
LAST = TILES - 1
QUADRANTS = 4
HALF = S // 2
HALVES = [slice(0, HALF), slice(HALF, S)]
BLOCKS = [slice(b * P, (b + 1) * P) for b in range(S // P)]
WHOLE = slice(0, S)
SUMMED_ON_TENSOR = 2


def tile_picked_joingatelseharm_none_po_kernel(
    tc, x_words, x_scales, w1_words, w1_scales, gn, gm, w2_words, w2_scales, w3_words, w3_scales,
    offs, n1, n2, n3, n4, out_0, out_1, out_2,
):
    nc = tc.nc
    with ExitStack() as ctx:
        keep = ctx.enter_context(tc.tile_pool(name="keep", bufs=1))
        psum = ctx.enter_context(tc.psum_pool(name="psum", bufs=1))

        def tile(name, shape, dtype, after=None):
            return keep.tile(shape, dtype, name=name, tag=after or name, align_bytes=64)

        def bank(name, number, width):
            return psum.tile([P, width], F32, name=name, tag="bank%d" % number)

        def load_list(name, src):
            offsets = keep.tile([P, S // 16], U16, name=name)
            nc.sync.dma_start(offsets[:], src)
            return offsets

        def entries(offsets, c):
            return offsets[:, c * HALF // 16 : (c + 1) * HALF // 16]

        def scale_plane(name, width):
            plane = tile(name, [P, width], U8)
            nc.vector.memset(plane[:].bitcast(I32), 0)
            return plane

        def load_scale_rows(plane, src, quadrants):
            for q in quadrants:
                nc.sync.dma_start(plane[32 * q : 32 * q + 4, :].bitcast(I32), src[0, 4 * q : 4 * q + 4, :].bitcast(I32))

        def load_words(name, src):
            words = tile(name, [P, src.shape[2]], U8)
            nc.sync.dma_start(words[:].bitcast(I32), src[0].bitcast(I32))
            return words

        def load_gain(name, src):
            gain = tile(name, [P, TILES], F32)
            nc.sync.dma_start(gain[:], src.rearrange("(p t) o -> p (t o)", t=TILES))
            return gain

        def deal_words(name, words):
            dealt = tile(name, [P, TILES, 2 * P], U8)
            nc.vector.tensor_copy(
                dealt[:].rearrange("p t (m b) -> p t m b", b=2),
                words[:].rearrange("p (m t b) -> p t m b", t=TILES, b=2),
            )
            return dealt

        def deal_scales(name, plane, tiles):
            dealt = tile(name, [P, len(tiles), P], U8)
            by_tile = plane[:].rearrange("p (m t) -> p t m", t=TILES)
            nc.vector.tensor_copy(dealt[:], by_tile[:, tiles.start : tiles.stop, :])
            return dealt

        def interleave(copy, dst, src):
            copy(dst.rearrange("p (c i) t -> p c t i", i=4), src.rearrange("p t (c i) -> p c t i", i=4))

        def quantise(codes, scales, interleaved):
            nc.vector.quantize_mx(codes.bitcast(FP8X4), scales, interleaved.rearrange("p c t -> p (c t)"))

        xs_plane = scale_plane("xs_plane", T)
        w1s_plane = scale_plane("w1s_plane", H)
        w2s_plane = scale_plane("w2s_plane", N)
        w3s_plane = scale_plane("w3s_plane", N)
        offs_t = load_list("offs_t", offs)
        w1_raw = load_words("w1_raw", w1_words)
        load_scale_rows(xs_plane, x_scales, range(QUADRANTS))
        load_scale_rows(w1s_plane, w1_scales, range(1))
        xw_table = tile("xw_table", [P, T], I32)
        nc.sync.dma_start(xw_table[:], x_words[0].rearrange("p n r -> p (n r)").bitcast(I32))
        load_scale_rows(w1s_plane, w1_scales, range(1, QUADRANTS))
        identity = tile("identity", [P, P], F32)
        make_identity(nc, identity[:])
        w2_raw = load_words("w2_raw", w2_words)
        w3_raw = load_words("w3_raw", w3_words)
        load_scale_rows(w2s_plane, w2_scales, range(QUADRANTS))
        n1_t = load_list("n1_t", n1)
        gn_t = load_gain("gn_t", gn)
        n2_t = load_list("n2_t", n2)
        gm_t = load_gain("gm_t", gm)
        n3_t = load_list("n3_t", n3)
        load_scale_rows(w3s_plane, w3_scales, range(QUADRANTS))
        n4_t = load_list("n4_t", n4)

        w1_c = deal_words("w1_c", w1_raw)
        xs = [tile("xs%d" % c, [P, HALF], U8) for c in range(2)]
        xw = [tile("xw%d" % c, [P, HALF], U32) for c in range(2)]
        for c in range(2):
            nc.vector.tensor_copy(xs[c][:], xs_plane[:].indirect(entries(offs_t, c)))
        nc.vector.tensor_copy(xw[0][:], xw_table[:].bitcast(U32).indirect(entries(offs_t, 0)))
        w1s_first = deal_scales("w1s_first", w1s_plane, range(1))
        nc.vector.tensor_copy(xw[1][:], xw_table[:].bitcast(U32).indirect(entries(offs_t, 1)))
        w1s_rest = deal_scales("w1s_rest", w1s_plane, range(1, TILES))
        w1_s = [w1s_first[:, 0, :]] + [w1s_rest[:, t, :] for t in range(LAST)]

        y_ps = [bank("y_ps%d" % t, t, S) for t in range(TILES)]
        for t in range(TILES):
            for c in range(2):
                nc.tensor.matmul_mx(
                    out=y_ps[t][:, HALVES[c]], lhsT=w1_c[:, t, :].bitcast(FP4X4), lhsT_scale=w1_s[t],
                    rhs=xw[c][:].bitcast(FP8X4), rhs_scale=xs[c][:], start=True, stop=True,
                )

        tanh_y = [tile("tanh_y%d" % t, [P, S], F32) for t in range(TILES)]
        y_ex = [tile("y_ex%d" % t, [P, 2 * S], F32) for t in range(TILES)]
        gate = [tile("gate%d" % t, [P, S], F32) for t in range(TILES)]
        ex_n2 = [tile("ex_n2_%d" % t, [P, S], F32) for t in range(TILES)]
        ex_sum = tile("ex_sum", [P, TILES, S], F32)
        z_tiles = tile("z_tiles", [P, TILES, S], BF16)

        def fetch_gate(t):
            nc.scalar.activation(tanh_y[t][:], y_ps[t][:], ACT.Tanh, scale=0.5)
            for c in range(2):
                nc.vector.tensor_scalar(
                    gate[t][:, HALVES[c]], tanh_y[t][:].indirect(entries(n1_t, c)), 0.5, 0.5, ALU.mult, ALU.add
                )

        def apply_gate(t):
            copy = nc.vector.tensor_copy if t == LAST else nc.scalar.copy
            copy(y_ex[t][:, :S], y_ps[t][:])
            nc.vector.scalar_tensor_tensor(z_tiles[:, t, :], y_ex[t][:, :S], gn_t[:, t : t + 1], gate[t][:], ALU.mult, ALU.mult)

        fetch_gate(0)
        for t in range(1, TILES):
            fetch_gate(t)
            apply_gate(t - 1)
        apply_gate(LAST)

        for t in range(TILES):
            nc.scalar.activation(y_ex[t][:, S:], y_ps[t][:], ACT.Exp)
            nc.scalar.activation(ex_n2[t][:], y_ex[t][:].indirect(n2_t[:]), ACT.Exp)
            nc.vector.tensor_tensor(ex_sum[:, t, :], y_ex[t][:, S:], ex_n2[t][:], ALU.add)

        minus_gm = tile("minus_gm", [P, TILES], F32)
        nc.scalar.activation(minus_gm[:], gm_t[:], ACT.Copy, scale=-1.0)
        w2_c = deal_words("w2_c", w2_raw)
        w3_c = deal_words("w3_c", w3_raw)
        z_woven = tile("z_woven", [P, S, TILES], BF16)
        interleave(nc.vector.tensor_copy, z_woven[:], z_tiles[:])
        w2_s = deal_scales("w2_s", w2s_plane, range(TILES))
        z_c = tile("z_c", [P, S], U32)
        z_s = tile("z_s", [P, S], U8)
        quantise(z_c[:], z_s[:], z_woven[:])
        w3_s = deal_scales("w3_s", w3s_plane, range(TILES))

        z2_c = [tile("z2_c%d" % c, [P, HALF], U32) for c in range(2)]
        z2_s = [tile("z2_s%d" % c, [P, HALF], U8) for c in range(2)]
        z2_tiles = [tile("z2_tiles%d" % c, [P, TILES, HALF], BF16) for c in range(2)]
        z2_woven = [tile("z2_woven%d" % c, [P, HALF, TILES], BF16) for c in range(2)]
        h_ps = [[bank("h_ps%d_%d" % (c, t), TILES * (1 - c) + t, HALF) for t in range(TILES)] for c in range(2)]
        h_sq = tile("h_sq", [P, TILES, S], F32)
        log_sum = tile("log_sum", [P, 2 * TILES, HALF], F32, after="ex_n2_%d" % LAST)
        taken_over = {(1, LAST - 1): "diff0_%d" % LAST, (1, LAST): "z2_tiles0"}

        def make_z2(c, t):
            diff = tile("diff%d_%d" % (c, t), [P, HALF], F32, after=taken_over.get((c, t)))
            nc.vector.tensor_tensor(diff[:], y_ex[t][:].indirect(entries(n3_t, c)), log_sum[:, TILES * c + t, :], ALU.subtract)
            if (c, t) == (1, LAST):
                nc.vector.tensor_scalar(z2_tiles[c][:, t, :], diff[:], minus_gm[:, t : t + 1], None, ALU.mult)
            else:
                nc.scalar.activation(z2_tiles[c][:, t, :], diff[:], ACT.Copy, scale=minus_gm[:, t : t + 1])

        def make_h(c):
            interleave(nc.vector.tensor_copy, z2_woven[c][:], z2_tiles[c][:])
            quantise(z2_c[c][:], z2_s[c][:], z2_woven[c][:])
            for t in range(TILES):
                for b in range(HALF // P):
                    in_half, in_all = BLOCKS[b], BLOCKS[HALF // P * c + b]
                    nc.tensor.matmul_mx(
                        out=h_ps[c][t][:, in_half], lhsT=w2_c[:, t, :].bitcast(FP4X4), lhsT_scale=w2_s[:, t, :],
                        rhs=z_c[:, in_all].bitcast(FP8X4), rhs_scale=z_s[:, in_all], start=True, stop=False,
                    )
                    nc.tensor.matmul_mx(
                        out=h_ps[c][t][:, in_half], lhsT=w3_c[:, t, :].bitcast(FP4X4), lhsT_scale=w3_s[:, t, :],
                        rhs=z2_c[c][:, in_half].bitcast(FP8X4), rhs_scale=z2_s[c][:, in_half], start=False, stop=True,
                    )

        for c in range(2):
            for t in range(TILES):
                nc.scalar.activation(log_sum[:, TILES * c + t, :], ex_sum[:, t, HALVES[c]], ACT.Ln)
        for t in range(TILES):
            make_z2(0, t)
        for t in range(LAST - 1):
            make_z2(1, t)
        make_h(0)
        for t in range(LAST - 1, TILES):
            make_z2(1, t)
        sixteen = tile("sixteen", [P, 1], F32)
        nc.vector.memset(sixteen[:], 16.0)
        quarter = tile("quarter", [P, 1], F32, after=taken_over[(1, LAST - 1)])
        nc.scalar.activation(quarter[:], sixteen[:], ACT.Abs_reciprocal_sqrt)
        make_h(1)

        h = [tile("h%d" % t, [P, S], F32) for t in range(TILES)]
        for t in range(TILES):
            nc.scalar.activation(h_sq[:, t, HALVES[0]], h_ps[0][t][:], ACT.Square)
        for t in range(TILES):
            nc.vector.tensor_copy(h[t][:, HALVES[0]], h_ps[0][t][:])
        for t in range(TILES):
            nc.scalar.copy(h[t][:, HALVES[1]], h_ps[1][t][:])

        out_c = tile("out_c", [P, S], U32)
        out_s = tile("out_s", [P, S], U8)
        out_rows = out_0.rearrange("(p t) c -> p t c", t=TILES)
        out_words = out_1[0].rearrange("p n r -> p (n r)").bitcast(I32)
        result = tile("result", [P, TILES, S], F32)
        pa = [tile("pa%d" % t, [P, S], F32) for t in range(TILES)]
        squares, factor, product = {}, {}, {}

        def fetch_pa(t):
            nc.scalar.activation(h_sq[:, t, HALVES[1]], h_ps[1][t][:], ACT.Square)
            for c in range(2):
                nc.vector.tensor_copy(pa[t][:, HALVES[c]], h[t][:].indirect(entries(n4_t, c)))
            pa_sq = tile("pa_sq%d" % t, [P, S], F32)
            nc.scalar.activation(pa_sq[:], pa[t][:], ACT.Square)
            if t >= SUMMED_ON_TENSOR:
                squares[t] = tile("squares%d" % t, [P, S], F32)
                nc.vector.tensor_tensor(squares[t][:], h_sq[:, t, :], pa_sq[:], ALU.add)
                return
            squares[t] = bank("squares_ps%d" % t, TILES + t, S)
            for blk in BLOCKS:
                nc.tensor.matmul(
                    squares[t][:, blk], h_sq[:, t, blk], identity[:], start=blk == BLOCKS[0], stop=False, is_transpose=True
                )
            for blk in BLOCKS:
                nc.tensor.matmul(
                    squares[t][:, blk], pa_sq[:, blk], identity[:], start=False, stop=blk == BLOCKS[-1], is_transpose=True
                )

        def invert(t):
            root = tile("root%d" % t, [P, S], F32)
            factor[t] = tile("factor%d" % t, [P, S], F32)
            for part in HALVES if t >= SUMMED_ON_TENSOR else [WHOLE]:
                nc.scalar.activation(root[:, part], squares[t][:, part], ACT.Abs_reciprocal_sqrt, scale=0.5, bias=quarter[:])
                nc.scalar.activation(factor[t][:, part], root[:, part], ACT.Square)
            if t < SUMMED_ON_TENSOR:
                transposed = factor[t]
                factor[t] = bank("factor_ps%d" % t, t, S)
                for blk in BLOCKS:
                    nc.tensor.transpose(factor[t][:, blk], transposed[:, blk], identity[:])

        def finish(t, part):
            nc.vector.tensor_tensor(result[:, t, part], product[t][:, part], factor[t][:, part], ALU.mult)
            nc.sync.dma_start(out_rows[:, t, part], result[:, t, part])

        fetch_pa(0)
        for t in range(1, TILES):
            fetch_pa(t)
            invert(t - 1)
        invert(LAST)
        for t in range(TILES):
            product[t] = tile("product%d" % t, [P, S], F32, after="pa_sq%d" % t)
            nc.vector.tensor_tensor(product[t][:], h[t][:], pa[t][:], ALU.mult)
        for t in range(LAST):
            finish(t, WHOLE)
        for part in HALVES:
            finish(LAST, part)

        woven = [tile("woven%d" % c, [P, HALF, TILES], BF16) for c in range(2)]
        interleave(nc.vector.tensor_copy, woven[0][:], result[:, :, HALVES[0]])
        interleave(nc.vector.tensor_copy, woven[1][:, :P, :], result[:, :, BLOCKS[-2]])
        interleave(nc.scalar.copy, woven[1][:, P:, :], result[:, :, BLOCKS[-1]])
        for c in range(2):
            quantise(out_c[:, HALVES[c]], out_s[:, HALVES[c]], woven[c][:])
            nc.sync.dma_start(out_words[:, HALVES[c]], out_c[:, HALVES[c]].bitcast(I32))
        for q in range(QUADRANTS):
            queue = nc.sync if q == QUADRANTS - 1 else nc.scalar
            queue.dma_start(out_2[0, 4 * q : 4 * q + 4, :].bitcast(I32), out_s[32 * q : 32 * q + 4, :].bitcast(I32))
